import numpy as np
import ml_dtypes


def mxq(x, axis, fmt="e4m3"):
    dtype, down = {"e4m3": (ml_dtypes.float8_e4m3fn, 7), "e5m2": (ml_dtypes.float8_e5m2, 14)}[fmt]
    v = np.moveaxis(np.asarray(x, np.float32).astype(ml_dtypes.bfloat16).astype(np.float64), axis, -1)
    blocks = v.reshape(v.shape[:-1] + (-1, 32))
    amax = np.abs(blocks).max(-1, keepdims=True)
    byte = np.maximum(np.where(amax > 0, np.frexp(amax)[1] - 1 + 127, 0) - down, 1)
    scale = np.exp2(byte - 127.0)
    codes = (blocks / scale).astype(np.float32).astype(dtype).astype(np.float64)
    return np.moveaxis((codes * scale).reshape(v.shape), -1, axis)


WIDE = False


def mx_kscale(k):
    if not WIDE:
        return np.ones(k)
    levels = np.array([10, -10, 5, -5, 0])
    if k % 512:
        return np.exp2(np.random.permutation(np.resize(levels, k // 32))).repeat(32)
    a = np.empty((k // 512, 16))
    for p in range(k // 512):
        a[p, :8] = np.random.permutation(np.resize(levels, 8))
        for g in range(8):
            far = levels[np.abs(levels - a[p, g]) >= 10]
            a[p, g + 8] = far[np.random.randint(len(far))]
    return np.exp2(a.ravel()).repeat(32)


def f64(x):
    return np.asarray(x).astype(np.float64)


def striped(idx):
    return np.tile(idx.reshape(-1, 16).T, (8, 1)).astype(np.uint16)


def unstriped(offs):
    return offs[:16].T.reshape(-1).astype(np.int64)


E2M1 = np.array([0.0, 0.5, 1.0, 1.5, 2.0, 3.0, 4.0, 6.0, -0.0, -0.5, -1.0, -1.5, -2.0, -3.0, -4.0, -6.0])


def pack_fp4(w):
    k, n = w.shape
    w = f64(np.asarray(w, np.float32).astype(ml_dtypes.bfloat16)).reshape(k // 32, 32, n)
    amax = np.abs(w).max(1)
    mant, ex = np.frexp(amax / 6.0)
    byte = np.clip(np.where(amax > 0, np.where(mant > 0.5, ex, ex - 1) + 127, 1), 1, 254)
    scaled = (w * np.exp2(127.0 - byte)[:, None, :]).reshape(k, n).astype(np.float32)
    c = np.ascontiguousarray(scaled.reshape(k // 512, 128, 4, n).transpose(0, 1, 3, 2)).astype(ml_dtypes.float4_e2m1fn).view(np.uint8) & 0xF
    words = (c[..., 0::2] | (c[..., 1::2] << 4)).reshape(k // 512, 128, 2 * n)
    return np.ascontiguousarray(words), np.ascontiguousarray(byte.astype(np.uint8).reshape(k // 512, 16, n))


def unpack_fp4(words, scales):
    g, _, n = scales.shape
    words = np.ascontiguousarray(words).reshape(g, 128, n, 2)
    nib = np.empty((g, 128, n, 4), np.uint8)
    nib[..., 0::2] = words & 0xF
    nib[..., 1::2] = words >> 4
    vals = E2M1[nib] * np.repeat(np.exp2(scales.astype(np.float64) - 127.0), 8, axis=1)[..., None]
    return vals.transpose(0, 1, 3, 2).reshape(g * 512, n)


def sigmoid(v):
    return 1.0 / (1.0 + np.exp(-np.maximum(v, -700.0)))


def gelu(v):
    return 0.5 * v * (1.0 + np.tanh(np.sqrt(2.0 / np.pi) * (v + 0.044715 * v**3)))


K, T, S, N = 512, 2048, 1024, 128


def setup_inputs():
    n = np.random.standard_normal
    s = mx_kscale(K)[:, None]
    packed_w1 = pack_fp4(n((K, N)) / np.sqrt(K) / s)
    packed_w2 = pack_fp4(n((K, N)) / np.sqrt(K) / s)
    return {
        "xT": (n((K, T)) * s).astype(np.float32),
        "res": n((N, T)).astype(np.float32),
        "w1_words": packed_w1[0],
        "w1_scales": packed_w1[1],
        "w2_words": packed_w2[0],
        "w2_scales": packed_w2[1],
        "offs": striped(np.random.permutation(T)[:S]),
    }


def reference(xT, res, w1_words, w1_scales, w2_words, w2_scales, offs):
    r = f64(res)[:, unstriped(offs)]
    xq = mxq(f64(xT)[:, unstriped(offs)], 0, "e4m3")
    g = sigmoid(unpack_fp4(w2_words, w2_scales).T @ xq)
    y = gelu(unpack_fp4(w1_words, w1_scales).T @ xq)
    return r + g * (y - r)

@@ -1,0 +1,139 @@
+from contextlib import ExitStack
+
+import concourse.mybir as mybir
+
+K, T, S, N = 512, 2048, 1024, 128
+FLOPS = 2 * 2 * K * S * N
+
+F32 = mybir.dt.float32
+BF16 = mybir.dt.bfloat16
+I32 = mybir.dt.int32
+U32 = mybir.dt.uint32
+U16 = mybir.dt.uint16
+U8 = mybir.dt.uint8
+FP8X4 = mybir.dt.float8_e4m3fn_x4
+FP4X4 = mybir.dt.float4_e2m1fn_x4
+ACT = mybir.ActivationFunctionType
+ALU = mybir.AluOpType
+
+P = 128
+CHUNK = 256
+CHUNKS = S // CHUNK
+LOW_LOADS = ((0, 1024, 352), (1024, 1024, 352))
+HIGH_LOADS = ((0, 1024, 704), (1024, 512, 0), (1536, 512, 176))
+
+
+def tile_picked_highway_gelu_l_kernel(tc, xT, res, w1_words, w1_scales, w2_words, w2_scales, offs, out):
+    nc = tc.nc
+    x_rows = xT.rearrange("(p j) t -> p j t", j=4)
+
+    with ExitStack() as ctx:
+        keep = ctx.enter_context(tc.tile_pool(name="keep", bufs=1))
+        psum = ctx.enter_context(tc.psum_pool(name="psum", bufs=1))
+
+        offsets = keep.tile([P, S // 16], U16, name="offsets")
+        res_sb = keep.tile([P, T], F32, name="res_sb")
+        words = [keep.tile([P, 2 * N], U8, name="words%d" % i, align_bytes=64) for i in range(2)]
+        scales = [keep.tile([P, N], U8, name="scales%d" % i, align_bytes=64) for i in range(2)]
+        pairs = [keep.tile([P, 2 * T], BF16, name="pairs%d" % h) for h in range(2)]
+        zero = keep.tile([P, 1], F32, name="zero")
+        zero_bias = keep.tile([P, 1], F32, name="zero_bias")
+
+        nc.vector.memset(zero[:], 0.0)
+        nc.scalar.activation(zero_bias[:], zero[:], ACT.Gelu_apprx_tanh)
+
+        def load_pair(h, first, width):
+            raw = keep.tile([P, 2, width], F32, name="raw%d_%d" % (h, first))
+            nc.sync.dma_start(out=raw[:], in_=x_rows[:, 2 * h : 2 * h + 2, first : first + width])
+            return raw
+
+        def cast_pair(h, raw, first, width, on_scalar):
+            dst = pairs[h][:].rearrange("p (c e) -> p c e", e=2)
+            src = raw[:].rearrange("p e c -> p c e")
+            if on_scalar > 0:
+                nc.scalar.copy(dst[:, first : first + on_scalar, :], src[:, 0:on_scalar, :])
+            if on_scalar < width:
+                nc.vector.tensor_copy(dst[:, first + on_scalar : first + width, :], src[:, on_scalar:width, :])
+
+        low_raw = [load_pair(0, first, width) for first, width, on_scalar in LOW_LOADS]
+        nc.sync.dma_start(offsets[:], offs)
+        for tile, dram in zip(words, (w1_words, w2_words)):
+            nc.sync.dma_start(out=tile[:].bitcast(I32), in_=dram[0].bitcast(I32))
+        for tile, dram, queue in zip(scales, (w1_scales, w2_scales), (nc.sync, nc.gpsimd)):
+            nc.vector.memset(tile[:].bitcast(I32), 0)
+            for q in range(4):
+                queue.dma_start(
+                    out=tile[32 * q : 32 * q + 4, :].bitcast(I32),
+                    in_=dram[0][4 * q : 4 * q + 4, :].bitcast(I32),
+                )
+        high_raw = [load_pair(1, first, width) for first, width, on_scalar in HIGH_LOADS]
+        nc.sync.dma_start(out=res_sb[:], in_=res)
+
+        passing = keep.tile([P, S], F32, name="passing")
+        picked = [keep.tile([P, 2, CHUNK], U32, name="picked%d" % c) for c in range(CHUNKS)]
+
+        def gather(h, c):
+            entries = offsets[:, c * CHUNK // 16 : (c + 1) * CHUNK // 16]
+            nc.vector.tensor_copy(picked[c][:, h, :], pairs[h][:].bitcast(U32).indirect(entries))
+
+        for raw, load in zip(low_raw, LOW_LOADS):
+            cast_pair(0, raw, *load)
+        for c in range(CHUNKS):
+            gather(0, c)
+        for raw, load in zip(high_raw, HIGH_LOADS):
+            cast_pair(1, raw, *load)
+
+        woven = [keep.tile([P, 4 * CHUNK], BF16, name="woven%d" % c, align_bytes=64) for c in range(CHUNKS)]
+        codes = [keep.tile([P, CHUNK], U32, name="codes%d" % c, align_bytes=64) for c in range(CHUNKS)]
+        x_scales = [keep.tile([P, CHUNK], U8, name="x_scales%d" % c, align_bytes=64) for c in range(CHUNKS)]
+        sums = [psum.tile([P, 2, CHUNK], F32, name="sums%d" % c) for c in range(CHUNKS)]
+        layer = [keep.tile([P, CHUNK], F32, name="layer%d" % c) for c in range(CHUNKS)]
+        half_tanh = [keep.tile([P, CHUNK], F32, name="half_tanh%d" % c) for c in range(CHUNKS)]
+        diff = [keep.tile([P, CHUNK], F32, name="diff%d" % c) for c in range(CHUNKS)]
+        gated = [keep.tile([P, CHUNK], F32, name="gated%d" % c) for c in range(CHUNKS)]
+        result = [keep.tile([P, CHUNK], F32, name="result%d" % c) for c in range(CHUNKS)]
+
+        def weave(c):
+            nc.scalar.copy(
+                woven[c][:].bitcast(U32).rearrange("p (c h) -> p c h", h=2),
+                picked[c][:].rearrange("p h c -> p c h"),
+            )
+
+        def multiply(c):
+            nc.vector.quantize_mx(out=codes[c][:].bitcast(FP8X4), scales=x_scales[c][:], in_=woven[c][:])
+            for i in range(2):
+                nc.tensor.matmul_mx(
+                    out=sums[c][:, i, :],
+                    lhsT=words[i][:].bitcast(FP4X4),
+                    lhsT_scale=scales[i][:],
+                    rhs=codes[c][:].bitcast(FP8X4),
+                    rhs_scale=x_scales[c][:],
+                    start=True,
+                    stop=True,
+                )
+
+        def activate(c):
+            nc.scalar.activation(layer[c][:], sums[c][:, 0, :], ACT.Gelu_apprx_tanh, bias=zero_bias[:])
+            nc.scalar.activation(half_tanh[c][:], sums[c][:, 1, :], ACT.Tanh, scale=0.5)
+
+        def mix(group):
+            for c in group:
+                nc.vector.tensor_tensor(diff[c][:], layer[c][:], passing[:, c * CHUNK : (c + 1) * CHUNK], ALU.subtract)
+            for c in group:
+                nc.vector.scalar_tensor_tensor(gated[c][:], half_tanh[c][:], 1.0, diff[c][:], ALU.add, ALU.mult)
+            for c in group:
+                cols = slice(c * CHUNK, (c + 1) * CHUNK)
+                nc.vector.scalar_tensor_tensor(result[c][:], gated[c][:], 0.5, passing[:, cols], ALU.mult, ALU.add)
+                nc.sync.dma_start(out=out[:, cols], in_=result[c][:])
+
+        for step in range(CHUNKS + 2):
+            if step < CHUNKS:
+                gather(1, step)
+                weave(step)
+            if 1 <= step <= CHUNKS:
+                multiply(step - 1)
+            if 2 <= step:
+                activate(step - 2)
+        nc.vector.tensor_copy(passing[:], res_sb[:].indirect(offsets[:]))
+        mix((0, 1))
+        mix((2, 3))

@@ -19,8 +19,10 @@ ALU = mybir.AluOpType
 P = 128
 CHUNK = 256
 CHUNKS = S // CHUNK
-LOW_LOADS = ((0, 1024, 352), (1024, 1024, 352))
-HIGH_LOADS = ((0, 1024, 704), (1024, 512, 0), (1536, 512, 176))
+VECTOR_CHUNKS = (3,)
+SCALAR_CHUNKS = (0, 1, 2)
+PAIR_LOADS = ((0, 1024, 0), (1024, 512, 0), (1536, 512, 176))
+LAST_LOAD = 512
 
 
 def tile_picked_highway_gelu_l_kernel(tc, xT, res, w1_words, w1_scales, w2_words, w2_scales, offs, out):
@@ -35,55 +37,65 @@ def tile_picked_highway_gelu_l_kernel(tc, xT, res, w1_words, w1_scales, w2_words
         res_sb = keep.tile([P, T], F32, name="res_sb")
         words = [keep.tile([P, 2 * N], U8, name="words%d" % i, align_bytes=64) for i in range(2)]
         scales = [keep.tile([P, N], U8, name="scales%d" % i, align_bytes=64) for i in range(2)]
-        pairs = [keep.tile([P, 2 * T], BF16, name="pairs%d" % h) for h in range(2)]
+        pairs = keep.tile([P, 2 * T], BF16, name="pairs")
+        row_f32 = {j: keep.tile([P, T], F32, name="row_f32_%d" % j) for j in (2, 3)}
+        row_bf16 = {j: keep.tile([P, T], BF16, name="row_bf16_%d" % j) for j in (2, 3)}
         zero = keep.tile([P, 1], F32, name="zero")
         zero_bias = keep.tile([P, 1], F32, name="zero_bias")
 
         nc.vector.memset(zero[:], 0.0)
         nc.scalar.activation(zero_bias[:], zero[:], ACT.Gelu_apprx_tanh)
 
-        def load_pair(h, first, width):
-            raw = keep.tile([P, 2, width], F32, name="raw%d_%d" % (h, first))
-            nc.sync.dma_start(out=raw[:], in_=x_rows[:, 2 * h : 2 * h + 2, first : first + width])
-            return raw
+        def entries(c):
+            return offsets[:, c * CHUNK // 16 : (c + 1) * CHUNK // 16]
 
-        def cast_pair(h, raw, first, width, on_scalar):
-            dst = pairs[h][:].rearrange("p (c e) -> p c e", e=2)
-            src = raw[:].rearrange("p e c -> p c e")
-            if on_scalar > 0:
-                nc.scalar.copy(dst[:, first : first + on_scalar, :], src[:, 0:on_scalar, :])
-            if on_scalar < width:
-                nc.vector.tensor_copy(dst[:, first + on_scalar : first + width, :], src[:, on_scalar:width, :])
-
-        low_raw = [load_pair(0, first, width) for first, width, on_scalar in LOW_LOADS]
+        nc.sync.dma_start(out=row_f32[2][:], in_=x_rows[:, 2, :])
         nc.sync.dma_start(offsets[:], offs)
         for tile, dram in zip(words, (w1_words, w2_words)):
             nc.sync.dma_start(out=tile[:].bitcast(I32), in_=dram[0].bitcast(I32))
-        for tile, dram, queue in zip(scales, (w1_scales, w2_scales), (nc.sync, nc.gpsimd)):
-            nc.vector.memset(tile[:].bitcast(I32), 0)
+        raw = []
+        for first, width, on_scalar in PAIR_LOADS:
+            piece = keep.tile([P, 2, width], F32, name="raw%d" % first)
+            nc.sync.dma_start(out=piece[:], in_=x_rows[:, 0:2, first : first + width])
+            raw.append(piece)
+        for first in range(0, T, LAST_LOAD):
+            nc.sync.dma_start(out=row_f32[3][:, first : first + LAST_LOAD], in_=x_rows[:, 3, first : first + LAST_LOAD])
+        nc.sync.dma_start(out=res_sb[:], in_=res)
+        for tile, dram in zip(scales, (w1_scales, w2_scales)):
             for q in range(4):
-                queue.dma_start(
+                nc.gpsimd.dma_start(
                     out=tile[32 * q : 32 * q + 4, :].bitcast(I32),
                     in_=dram[0][4 * q : 4 * q + 4, :].bitcast(I32),
                 )
-        high_raw = [load_pair(1, first, width) for first, width, on_scalar in HIGH_LOADS]
-        nc.sync.dma_start(out=res_sb[:], in_=res)
-
-        passing = keep.tile([P, S], F32, name="passing")
-        picked = [keep.tile([P, 2, CHUNK], U32, name="picked%d" % c) for c in range(CHUNKS)]
-
-        def gather(h, c):
-            entries = offsets[:, c * CHUNK // 16 : (c + 1) * CHUNK // 16]
-            nc.vector.tensor_copy(picked[c][:, h, :], pairs[h][:].bitcast(U32).indirect(entries))
-
-        for raw, load in zip(low_raw, LOW_LOADS):
-            cast_pair(0, raw, *load)
-        for c in range(CHUNKS):
-            gather(0, c)
-        for raw, load in zip(high_raw, HIGH_LOADS):
-            cast_pair(1, raw, *load)
 
         woven = [keep.tile([P, 4 * CHUNK], BF16, name="woven%d" % c, align_bytes=64) for c in range(CHUNKS)]
+
+        def gather_row(j, c):
+            slot = woven[c][:].rearrange("p (c t) -> p c t", t=4)[:, :, j]
+            if c in VECTOR_CHUNKS:
+                nc.vector.tensor_copy(slot, row_f32[j][:].indirect(entries(c)))
+            else:
+                nc.scalar.activation(slot, row_bf16[j][:].indirect(entries(c)), ACT.Copy)
+
+        nc.vector.tensor_copy(row_bf16[2][:], row_f32[2][:])
+        for c in range(CHUNKS):
+            gather_row(2, c)
+
+        dst = pairs[:].rearrange("p (c e) -> p c e", e=2)
+        for piece, (first, width, on_scalar) in zip(raw, PAIR_LOADS):
+            src = piece[:].rearrange("p e c -> p c e")
+            if on_scalar > 0:
+                nc.scalar.copy(dst[:, first : first + on_scalar, :], src[:, 0:on_scalar, :])
+            nc.vector.tensor_copy(dst[:, first + on_scalar : first + width, :], src[:, on_scalar:width, :])
+        for c in range(CHUNKS):
+            low_words = woven[c][:].bitcast(U32).rearrange("p (c h) -> p c h", h=2)[:, :, 0]
+            nc.vector.tensor_copy(low_words, pairs[:].bitcast(U32).indirect(entries(c)))
+
+        for first in range(0, T, LAST_LOAD):
+            nc.scalar.copy(row_bf16[3][:, first : first + LAST_LOAD], row_f32[3][:, first : first + LAST_LOAD])
+        for c in range(CHUNKS):
+            gather_row(3, c)
+
         codes = [keep.tile([P, CHUNK], U32, name="codes%d" % c, align_bytes=64) for c in range(CHUNKS)]
         x_scales = [keep.tile([P, CHUNK], U8, name="x_scales%d" % c, align_bytes=64) for c in range(CHUNKS)]
         sums = [psum.tile([P, 2, CHUNK], F32, name="sums%d" % c) for c in range(CHUNKS)]
@@ -92,12 +104,6 @@ def tile_picked_highway_gelu_l_kernel(tc, xT, res, w1_words, w1_scales, w2_words
         diff = [keep.tile([P, CHUNK], F32, name="diff%d" % c) for c in range(CHUNKS)]
         gated = [keep.tile([P, CHUNK], F32, name="gated%d" % c) for c in range(CHUNKS)]
         result = [keep.tile([P, CHUNK], F32, name="result%d" % c) for c in range(CHUNKS)]
-
-        def weave(c):
-            nc.scalar.copy(
-                woven[c][:].bitcast(U32).rearrange("p (c h) -> p c h", h=2),
-                picked[c][:].rearrange("p h c -> p c h"),
-            )
 
         def multiply(c):
             nc.vector.quantize_mx(out=codes[c][:].bitcast(FP8X4), scales=x_scales[c][:], in_=woven[c][:])
@@ -118,22 +124,17 @@ def tile_picked_highway_gelu_l_kernel(tc, xT, res, w1_words, w1_scales, w2_words
 
         def mix(group):
             for c in group:
-                nc.vector.tensor_tensor(diff[c][:], layer[c][:], passing[:, c * CHUNK : (c + 1) * CHUNK], ALU.subtract)
+                nc.vector.tensor_tensor(diff[c][:], res_sb[:].indirect(entries(c)), layer[c][:], ALU.subtract)
             for c in group:
-                nc.vector.scalar_tensor_tensor(gated[c][:], half_tanh[c][:], 1.0, diff[c][:], ALU.add, ALU.mult)
+                nc.vector.scalar_tensor_tensor(gated[c][:], half_tanh[c][:], 1.0, diff[c][:], ALU.subtract, ALU.mult)
             for c in group:
                 cols = slice(c * CHUNK, (c + 1) * CHUNK)
-                nc.vector.scalar_tensor_tensor(result[c][:], gated[c][:], 0.5, passing[:, cols], ALU.mult, ALU.add)
+                nc.vector.scalar_tensor_tensor(result[c][:], gated[c][:], -0.5, layer[c][:], ALU.mult, ALU.add)
                 nc.sync.dma_start(out=out[:, cols], in_=result[c][:])
 
-        for step in range(CHUNKS + 2):
-            if step < CHUNKS:
-                gather(1, step)
-                weave(step)
-            if 1 <= step <= CHUNKS:
-                multiply(step - 1)
-            if 2 <= step:
-                activate(step - 2)
-        nc.vector.tensor_copy(passing[:], res_sb[:].indirect(offsets[:]))
+        for c in range(CHUNKS):
+            multiply(c)
+        for c in range(CHUNKS):
+            activate(c)
         mix((0, 1))
         mix((2, 3))

@@ -19,8 +19,7 @@ ALU = mybir.AluOpType
 P = 128
 CHUNK = 256
 CHUNKS = S // CHUNK
-VECTOR_CHUNKS = (3,)
-SCALAR_CHUNKS = (0, 1, 2)
+VECTOR_CHUNKS = (0,)
 PAIR_LOADS = ((0, 1024, 0), (1024, 512, 0), (1536, 512, 176))
 LAST_LOAD = 512
 
@@ -51,8 +50,6 @@ def tile_picked_highway_gelu_l_kernel(tc, xT, res, w1_words, w1_scales, w2_words
 
         nc.sync.dma_start(out=row_f32[2][:], in_=x_rows[:, 2, :])
         nc.sync.dma_start(offsets[:], offs)
-        for tile, dram in zip(words, (w1_words, w2_words)):
-            nc.sync.dma_start(out=tile[:].bitcast(I32), in_=dram[0].bitcast(I32))
         raw = []
         for first, width, on_scalar in PAIR_LOADS:
             piece = keep.tile([P, 2, width], F32, name="raw%d" % first)
@@ -60,6 +57,8 @@ def tile_picked_highway_gelu_l_kernel(tc, xT, res, w1_words, w1_scales, w2_words
             raw.append(piece)
         for first in range(0, T, LAST_LOAD):
             nc.sync.dma_start(out=row_f32[3][:, first : first + LAST_LOAD], in_=x_rows[:, 3, first : first + LAST_LOAD])
+        for tile, dram in zip(words, (w1_words, w2_words)):
+            nc.sync.dma_start(out=tile[:].bitcast(I32), in_=dram[0].bitcast(I32))
         nc.sync.dma_start(out=res_sb[:], in_=res)
         for tile, dram in zip(scales, (w1_scales, w2_scales)):
             for q in range(4):
@@ -96,45 +95,54 @@ def tile_picked_highway_gelu_l_kernel(tc, xT, res, w1_words, w1_scales, w2_words
         for c in range(CHUNKS):
             gather_row(3, c)
 
-        codes = [keep.tile([P, CHUNK], U32, name="codes%d" % c, align_bytes=64) for c in range(CHUNKS)]
-        x_scales = [keep.tile([P, CHUNK], U8, name="x_scales%d" % c, align_bytes=64) for c in range(CHUNKS)]
-        sums = [psum.tile([P, 2, CHUNK], F32, name="sums%d" % c) for c in range(CHUNKS)]
+        halves = CHUNKS // 2
+        codes = [keep.tile([P, 2 * CHUNK], U32, name="codes%d" % g, align_bytes=64) for g in range(halves)]
+        x_scales = [keep.tile([P, 2 * CHUNK], U8, name="x_scales%d" % g, align_bytes=64) for g in range(halves)]
+        layer_sums = [psum.tile([P, CHUNK], F32, name="layer_sums%d" % c) for c in range(CHUNKS)]
+        gate_sums = [psum.tile([P, 2 * CHUNK], F32, name="gate_sums%d" % g) for g in range(halves)]
+        half_tanh = [keep.tile([P, 2 * CHUNK], F32, name="half_tanh%d" % g) for g in range(halves)]
         layer = [keep.tile([P, CHUNK], F32, name="layer%d" % c) for c in range(CHUNKS)]
-        half_tanh = [keep.tile([P, CHUNK], F32, name="half_tanh%d" % c) for c in range(CHUNKS)]
         diff = [keep.tile([P, CHUNK], F32, name="diff%d" % c) for c in range(CHUNKS)]
         gated = [keep.tile([P, CHUNK], F32, name="gated%d" % c) for c in range(CHUNKS)]
         result = [keep.tile([P, CHUNK], F32, name="result%d" % c) for c in range(CHUNKS)]
 
-        def multiply(c):
-            nc.vector.quantize_mx(out=codes[c][:].bitcast(FP8X4), scales=x_scales[c][:], in_=woven[c][:])
-            for i in range(2):
-                nc.tensor.matmul_mx(
-                    out=sums[c][:, i, :],
-                    lhsT=words[i][:].bitcast(FP4X4),
-                    lhsT_scale=scales[i][:],
-                    rhs=codes[c][:].bitcast(FP8X4),
-                    rhs_scale=x_scales[c][:],
-                    start=True,
-                    stop=True,
-                )
+        def within_half(c):
+            return slice((c % 2) * CHUNK, (c % 2 + 1) * CHUNK)
 
-        def activate(c):
-            nc.scalar.activation(layer[c][:], sums[c][:, 0, :], ACT.Gelu_apprx_tanh, bias=zero_bias[:])
-            nc.scalar.activation(half_tanh[c][:], sums[c][:, 1, :], ACT.Tanh, scale=0.5)
-
-        def mix(group):
-            for c in group:
-                nc.vector.tensor_tensor(diff[c][:], res_sb[:].indirect(entries(c)), layer[c][:], ALU.subtract)
-            for c in group:
-                nc.vector.scalar_tensor_tensor(gated[c][:], half_tanh[c][:], 1.0, diff[c][:], ALU.subtract, ALU.mult)
-            for c in group:
-                cols = slice(c * CHUNK, (c + 1) * CHUNK)
-                nc.vector.scalar_tensor_tensor(result[c][:], gated[c][:], -0.5, layer[c][:], ALU.mult, ALU.add)
-                nc.sync.dma_start(out=out[:, cols], in_=result[c][:])
+        def product(sums, i, g, cols):
+            nc.tensor.matmul_mx(
+                out=sums[:],
+                lhsT=words[i][:].bitcast(FP4X4),
+                lhsT_scale=scales[i][:],
+                rhs=codes[g][:, cols].bitcast(FP8X4),
+                rhs_scale=x_scales[g][:, cols],
+                start=True,
+                stop=True,
+            )
 
         for c in range(CHUNKS):
-            multiply(c)
+            g, cols = c // 2, within_half(c)
+            nc.vector.quantize_mx(out=codes[g][:, cols].bitcast(FP8X4), scales=x_scales[g][:, cols], in_=woven[c][:])
+            product(layer_sums[c], 0, g, cols)
+            if c % 2 == 1:
+                product(gate_sums[g], 1, g, slice(0, 2 * CHUNK))
         for c in range(CHUNKS):
-            activate(c)
-        mix((0, 1))
-        mix((2, 3))
+            nc.scalar.activation(layer[c][:], layer_sums[c][:], ACT.Gelu_apprx_tanh, bias=zero_bias[:])
+            if c % 2 == 1:
+                nc.scalar.activation(half_tanh[c // 2][:], gate_sums[c // 2][:], ACT.Tanh, scale=0.5)
+
+        def subtract(c):
+            nc.vector.tensor_tensor(diff[c][:], res_sb[:].indirect(entries(c)), layer[c][:], ALU.subtract)
+
+        def gate(c):
+            t = half_tanh[c // 2][:, within_half(c)]
+            nc.vector.scalar_tensor_tensor(gated[c][:], t, 1.0, diff[c][:], ALU.subtract, ALU.mult)
+
+        def finish(c):
+            nc.vector.scalar_tensor_tensor(result[c][:], gated[c][:], -0.5, layer[c][:], ALU.mult, ALU.add)
+            nc.sync.dma_start(out=out[:, c * CHUNK : (c + 1) * CHUNK], in_=result[c][:])
+
+        for g in range(halves):
+            for step in (subtract, gate, finish):
+                step(2 * g)
+                step(2 * g + 1)

@@ -17,28 +17,30 @@ ACT = mybir.ActivationFunctionType
 ALU = mybir.AluOpType
 
 P = 128
+PACK = 4
+LIST_ROWS = 16
 CHUNK = 256
 CHUNKS = S // CHUNK
-VECTOR_CHUNKS = (0,)
-PAIR_LOADS = ((0, 1024, 0), (1024, 512, 0), (1536, 512, 176))
-LAST_LOAD = 512
+VECTOR_CHUNK = 0
+PAIR_LOADS = ((0, 1024, 0), (1024, 768, 256), (1792, 256, 88))
+LAST_ROW_LOAD = 512
 
 
 def tile_picked_highway_gelu_l_kernel(tc, xT, res, w1_words, w1_scales, w2_words, w2_scales, offs, out):
     nc = tc.nc
-    x_rows = xT.rearrange("(p j) t -> p j t", j=4)
+    x_rows = xT.rearrange("(p t) c -> p t c", t=PACK)
 
     with ExitStack() as ctx:
         keep = ctx.enter_context(tc.tile_pool(name="keep", bufs=1))
         psum = ctx.enter_context(tc.psum_pool(name="psum", bufs=1))
 
-        offsets = keep.tile([P, S // 16], U16, name="offsets")
+        offsets = keep.tile([P, S // LIST_ROWS], U16, name="offsets")
         res_sb = keep.tile([P, T], F32, name="res_sb")
-        words = [keep.tile([P, 2 * N], U8, name="words%d" % i, align_bytes=64) for i in range(2)]
-        scales = [keep.tile([P, N], U8, name="scales%d" % i, align_bytes=64) for i in range(2)]
+        w_words = [keep.tile([P, 2 * N], U8, name="w_words%d" % i, align_bytes=64) for i in range(2)]
+        w_scales = [keep.tile([P, N], U8, name="w_scales%d" % i, align_bytes=64) for i in range(2)]
         pairs = keep.tile([P, 2 * T], BF16, name="pairs")
-        row_f32 = {j: keep.tile([P, T], F32, name="row_f32_%d" % j) for j in (2, 3)}
-        row_bf16 = {j: keep.tile([P, T], BF16, name="row_bf16_%d" % j) for j in (2, 3)}
+        row_f32 = {t: keep.tile([P, T], F32, name="row_f32_%d" % t) for t in (2, 3)}
+        row_bf16 = {t: keep.tile([P, T], BF16, name="row_bf16_%d" % t) for t in (2, 3)}
         zero = keep.tile([P, 1], F32, name="zero")
         zero_bias = keep.tile([P, 1], F32, name="zero_bias")
 
@@ -46,61 +48,63 @@ def tile_picked_highway_gelu_l_kernel(tc, xT, res, w1_words, w1_scales, w2_words
         nc.scalar.activation(zero_bias[:], zero[:], ACT.Gelu_apprx_tanh)
 
         def entries(c):
-            return offsets[:, c * CHUNK // 16 : (c + 1) * CHUNK // 16]
+            return offsets[:, c * CHUNK // LIST_ROWS : (c + 1) * CHUNK // LIST_ROWS]
 
         nc.sync.dma_start(out=row_f32[2][:], in_=x_rows[:, 2, :])
         nc.sync.dma_start(offsets[:], offs)
-        raw = []
+        pair_pieces = []
         for first, width, on_scalar in PAIR_LOADS:
-            piece = keep.tile([P, 2, width], F32, name="raw%d" % first)
+            piece = keep.tile([P, 2, width], F32, name="pair_piece%d" % first)
             nc.sync.dma_start(out=piece[:], in_=x_rows[:, 0:2, first : first + width])
-            raw.append(piece)
-        for first in range(0, T, LAST_LOAD):
-            nc.sync.dma_start(out=row_f32[3][:, first : first + LAST_LOAD], in_=x_rows[:, 3, first : first + LAST_LOAD])
-        for tile, dram in zip(words, (w1_words, w2_words)):
+            pair_pieces.append(piece)
+        for first in range(0, T, LAST_ROW_LOAD):
+            cols = slice(first, first + LAST_ROW_LOAD)
+            nc.sync.dma_start(out=row_f32[3][:, cols], in_=x_rows[:, 3, cols])
+        for tile, dram in zip(w_words, (w1_words, w2_words)):
             nc.sync.dma_start(out=tile[:].bitcast(I32), in_=dram[0].bitcast(I32))
         nc.sync.dma_start(out=res_sb[:], in_=res)
-        for tile, dram in zip(scales, (w1_scales, w2_scales)):
+        for tile, dram in zip(w_scales, (w1_scales, w2_scales)):
             for q in range(4):
                 nc.gpsimd.dma_start(
                     out=tile[32 * q : 32 * q + 4, :].bitcast(I32),
                     in_=dram[0][4 * q : 4 * q + 4, :].bitcast(I32),
                 )
 
-        woven = [keep.tile([P, 4 * CHUNK], BF16, name="woven%d" % c, align_bytes=64) for c in range(CHUNKS)]
+        woven = [keep.tile([P, PACK * CHUNK], BF16, name="woven%d" % c, align_bytes=64) for c in range(CHUNKS)]
 
-        def gather_row(j, c):
-            slot = woven[c][:].rearrange("p (c t) -> p c t", t=4)[:, :, j]
-            if c in VECTOR_CHUNKS:
-                nc.vector.tensor_copy(slot, row_f32[j][:].indirect(entries(c)))
+        def gather_row(t, c):
+            place = woven[c][:].rearrange("p (e t) -> p e t", t=PACK)[:, :, t]
+            if c == VECTOR_CHUNK:
+                nc.vector.tensor_copy(place, row_f32[t][:].indirect(entries(c)))
             else:
-                nc.scalar.activation(slot, row_bf16[j][:].indirect(entries(c)), ACT.Copy)
+                nc.scalar.activation(place, row_bf16[t][:].indirect(entries(c)), ACT.Copy)
 
         nc.vector.tensor_copy(row_bf16[2][:], row_f32[2][:])
         for c in range(CHUNKS):
             gather_row(2, c)
 
-        dst = pairs[:].rearrange("p (c e) -> p c e", e=2)
-        for piece, (first, width, on_scalar) in zip(raw, PAIR_LOADS):
-            src = piece[:].rearrange("p e c -> p c e")
+        pairs_by_token = pairs[:].rearrange("p (c t) -> p c t", t=2)
+        for piece, (first, width, on_scalar) in zip(pair_pieces, PAIR_LOADS):
+            source = piece[:].rearrange("p t c -> p c t")
             if on_scalar > 0:
-                nc.scalar.copy(dst[:, first : first + on_scalar, :], src[:, 0:on_scalar, :])
-            nc.vector.tensor_copy(dst[:, first + on_scalar : first + width, :], src[:, on_scalar:width, :])
+                nc.scalar.copy(pairs_by_token[:, first : first + on_scalar, :], source[:, 0:on_scalar, :])
+            nc.vector.tensor_copy(pairs_by_token[:, first + on_scalar : first + width, :], source[:, on_scalar:width, :])
         for c in range(CHUNKS):
-            low_words = woven[c][:].bitcast(U32).rearrange("p (c h) -> p c h", h=2)[:, :, 0]
-            nc.vector.tensor_copy(low_words, pairs[:].bitcast(U32).indirect(entries(c)))
+            first_words = woven[c][:].bitcast(U32).rearrange("p (e h) -> p e h", h=2)[:, :, 0]
+            nc.vector.tensor_copy(first_words, pairs[:].bitcast(U32).indirect(entries(c)))
 
-        for first in range(0, T, LAST_LOAD):
-            nc.scalar.copy(row_bf16[3][:, first : first + LAST_LOAD], row_f32[3][:, first : first + LAST_LOAD])
+        for first in range(0, T, LAST_ROW_LOAD):
+            cols = slice(first, first + LAST_ROW_LOAD)
+            nc.scalar.copy(row_bf16[3][:, cols], row_f32[3][:, cols])
         for c in range(CHUNKS):
             gather_row(3, c)
 
         halves = CHUNKS // 2
-        codes = [keep.tile([P, 2 * CHUNK], U32, name="codes%d" % g, align_bytes=64) for g in range(halves)]
-        x_scales = [keep.tile([P, 2 * CHUNK], U8, name="x_scales%d" % g, align_bytes=64) for g in range(halves)]
+        x_codes = [keep.tile([P, 2 * CHUNK], U32, name="x_codes%d" % h, align_bytes=64) for h in range(halves)]
+        x_scales = [keep.tile([P, 2 * CHUNK], U8, name="x_scales%d" % h, align_bytes=64) for h in range(halves)]
         layer_sums = [psum.tile([P, CHUNK], F32, name="layer_sums%d" % c) for c in range(CHUNKS)]
-        gate_sums = [psum.tile([P, 2 * CHUNK], F32, name="gate_sums%d" % g) for g in range(halves)]
-        half_tanh = [keep.tile([P, 2 * CHUNK], F32, name="half_tanh%d" % g) for g in range(halves)]
+        gate_sums = [psum.tile([P, 2 * CHUNK], F32, name="gate_sums%d" % h) for h in range(halves)]
+        gate_tanh = [keep.tile([P, 2 * CHUNK], F32, name="gate_tanh%d" % h) for h in range(halves)]
         layer = [keep.tile([P, CHUNK], F32, name="layer%d" % c) for c in range(CHUNKS)]
         diff = [keep.tile([P, CHUNK], F32, name="diff%d" % c) for c in range(CHUNKS)]
         gated = [keep.tile([P, CHUNK], F32, name="gated%d" % c) for c in range(CHUNKS)]
@@ -109,40 +113,40 @@ def tile_picked_highway_gelu_l_kernel(tc, xT, res, w1_words, w1_scales, w2_words
         def within_half(c):
             return slice((c % 2) * CHUNK, (c % 2 + 1) * CHUNK)
 
-        def product(sums, i, g, cols):
+        def product(sums, i, h, cols):
             nc.tensor.matmul_mx(
                 out=sums[:],
-                lhsT=words[i][:].bitcast(FP4X4),
-                lhsT_scale=scales[i][:],
-                rhs=codes[g][:, cols].bitcast(FP8X4),
-                rhs_scale=x_scales[g][:, cols],
+                lhsT=w_words[i][:].bitcast(FP4X4),
+                lhsT_scale=w_scales[i][:],
+                rhs=x_codes[h][:, cols].bitcast(FP8X4),
+                rhs_scale=x_scales[h][:, cols],
                 start=True,
                 stop=True,
             )
 
         for c in range(CHUNKS):
-            g, cols = c // 2, within_half(c)
-            nc.vector.quantize_mx(out=codes[g][:, cols].bitcast(FP8X4), scales=x_scales[g][:, cols], in_=woven[c][:])
-            product(layer_sums[c], 0, g, cols)
+            h, cols = c // 2, within_half(c)
+            nc.vector.quantize_mx(out=x_codes[h][:, cols].bitcast(FP8X4), scales=x_scales[h][:, cols], in_=woven[c][:])
+            product(layer_sums[c], 0, h, cols)
             if c % 2 == 1:
-                product(gate_sums[g], 1, g, slice(0, 2 * CHUNK))
+                product(gate_sums[h], 1, h, slice(0, 2 * CHUNK))
         for c in range(CHUNKS):
             nc.scalar.activation(layer[c][:], layer_sums[c][:], ACT.Gelu_apprx_tanh, bias=zero_bias[:])
             if c % 2 == 1:
-                nc.scalar.activation(half_tanh[c // 2][:], gate_sums[c // 2][:], ACT.Tanh, scale=0.5)
+                nc.scalar.activation(gate_tanh[c // 2][:], gate_sums[c // 2][:], ACT.Tanh, scale=0.5)
 
         def subtract(c):
             nc.vector.tensor_tensor(diff[c][:], res_sb[:].indirect(entries(c)), layer[c][:], ALU.subtract)
 
         def gate(c):
-            t = half_tanh[c // 2][:, within_half(c)]
-            nc.vector.scalar_tensor_tensor(gated[c][:], t, 1.0, diff[c][:], ALU.subtract, ALU.mult)
+            a = gate_tanh[c // 2][:, within_half(c)]
+            nc.vector.scalar_tensor_tensor(gated[c][:], a, 1.0, diff[c][:], ALU.subtract, ALU.mult)
 
         def finish(c):
             nc.vector.scalar_tensor_tensor(result[c][:], gated[c][:], -0.5, layer[c][:], ALU.mult, ALU.add)
             nc.sync.dma_start(out=out[:, c * CHUNK : (c + 1) * CHUNK], in_=result[c][:])
 
-        for g in range(halves):
+        for h in range(halves):
             for step in (subtract, gate, finish):
-                step(2 * g)
-                step(2 * g + 1)
+                step(2 * h)
+                step(2 * h + 1)

@@ -21,9 +21,8 @@ PACK = 4
 LIST_ROWS = 16
 CHUNK = 256
 CHUNKS = S // CHUNK
-VECTOR_CHUNK = 0
-PAIR_LOADS = ((0, 1024, 0), (1024, 768, 256), (1792, 256, 88))
-LAST_ROW_LOAD = 512
+ROW_LOADS = ((0, 1536), (1536, 512))
+VECTOR_ENTRIES = (384, 384, CHUNK, CHUNK)
 
 
 def tile_picked_highway_gelu_l_kernel(tc, xT, res, w1_words, w1_scales, w2_words, w2_scales, offs, out):
@@ -38,30 +37,30 @@ def tile_picked_highway_gelu_l_kernel(tc, xT, res, w1_words, w1_scales, w2_words
         res_sb = keep.tile([P, T], F32, name="res_sb")
         w_words = [keep.tile([P, 2 * N], U8, name="w_words%d" % i, align_bytes=64) for i in range(2)]
         w_scales = [keep.tile([P, N], U8, name="w_scales%d" % i, align_bytes=64) for i in range(2)]
-        pairs = keep.tile([P, 2 * T], BF16, name="pairs")
-        row_f32 = {t: keep.tile([P, T], F32, name="row_f32_%d" % t) for t in (2, 3)}
-        row_bf16 = {t: keep.tile([P, T], BF16, name="row_bf16_%d" % t) for t in (2, 3)}
+        row_f32 = [keep.tile([P, T], F32, name="row_f32_%d" % t) for t in range(PACK)]
+        row_bf16 = [keep.tile([P, T], BF16, name="row_bf16_%d" % t) for t in range(PACK)]
+        woven = keep.tile([P, PACK * S], BF16, name="woven", align_bytes=64)
+        woven_by_entry = woven[:].rearrange("p (e t) -> p e t", t=PACK)
         zero = keep.tile([P, 1], F32, name="zero")
-        zero_bias = keep.tile([P, 1], F32, name="zero_bias")
+        tanh_bias = woven_by_entry[:, S - CHUNK, PACK - 1 : PACK]
 
         nc.vector.memset(zero[:], 0.0)
-        nc.scalar.activation(zero_bias[:], zero[:], ACT.Gelu_apprx_tanh)
+        nc.scalar.activation(tanh_bias, zero[:], ACT.Gelu_apprx_tanh)
 
-        def entries(c):
-            return offsets[:, c * CHUNK // LIST_ROWS : (c + 1) * CHUNK // LIST_ROWS]
+        def entries(first, end):
+            return offsets[:, first // LIST_ROWS : end // LIST_ROWS]
 
-        nc.sync.dma_start(out=row_f32[2][:], in_=x_rows[:, 2, :])
-        nc.sync.dma_start(offsets[:], offs)
-        pair_pieces = []
-        for first, width, on_scalar in PAIR_LOADS:
-            piece = keep.tile([P, 2, width], F32, name="pair_piece%d" % first)
-            nc.sync.dma_start(out=piece[:], in_=x_rows[:, 0:2, first : first + width])
-            pair_pieces.append(piece)
-        for first in range(0, T, LAST_ROW_LOAD):
-            cols = slice(first, first + LAST_ROW_LOAD)
-            nc.sync.dma_start(out=row_f32[3][:, cols], in_=x_rows[:, 3, cols])
-        for tile, dram in zip(w_words, (w1_words, w2_words)):
-            nc.sync.dma_start(out=tile[:].bitcast(I32), in_=dram[0].bitcast(I32))
+        def load_words(i, dram):
+            nc.sync.dma_start(out=w_words[i][:].bitcast(I32), in_=dram[0].bitcast(I32))
+
+        for t in range(PACK):
+            for first, width in ROW_LOADS:
+                cols = slice(first, first + width)
+                nc.sync.dma_start(out=row_f32[t][:, cols], in_=x_rows[:, t, cols])
+                if t == 0 and first == 0:
+                    nc.sync.dma_start(offsets[:], offs)
+        load_words(0, w1_words)
+        load_words(1, w2_words)
         nc.sync.dma_start(out=res_sb[:], in_=res)
         for tile, dram in zip(w_scales, (w1_scales, w2_scales)):
             for q in range(4):
@@ -70,83 +69,86 @@ def tile_picked_highway_gelu_l_kernel(tc, xT, res, w1_words, w1_scales, w2_words
                     in_=dram[0][4 * q : 4 * q + 4, :].bitcast(I32),
                 )
 
-        woven = [keep.tile([P, PACK * CHUNK], BF16, name="woven%d" % c, align_bytes=64) for c in range(CHUNKS)]
+        def gather_on_vector(t, first, end):
+            nc.vector.tensor_copy(woven_by_entry[:, first:end, t], row_f32[t][:].indirect(entries(first, end)))
 
-        def gather_row(t, c):
-            place = woven[c][:].rearrange("p (e t) -> p e t", t=PACK)[:, :, t]
-            if c == VECTOR_CHUNK:
-                nc.vector.tensor_copy(place, row_f32[t][:].indirect(entries(c)))
-            else:
-                nc.scalar.activation(place, row_bf16[t][:].indirect(entries(c)), ACT.Copy)
+        def gather_on_scalar(t, first, end):
+            nc.scalar.activation(woven_by_entry[:, first:end, t], row_bf16[t][:].indirect(entries(first, end)), ACT.Copy)
 
-        nc.vector.tensor_copy(row_bf16[2][:], row_f32[2][:])
-        for c in range(CHUNKS):
-            gather_row(2, c)
+        for t in range(PACK):
+            for first, width in ROW_LOADS:
+                cols = slice(first, first + width)
+                nc.vector.tensor_copy(row_bf16[t][:, cols], row_f32[t][:, cols])
+            gather_on_vector(t, 0, VECTOR_ENTRIES[t])
+            if t < PACK - 1:
+                gather_on_scalar(t, VECTOR_ENTRIES[t], S)
+        for c in range(1, CHUNKS - 1):
+            gather_on_scalar(PACK - 1, c * CHUNK, (c + 1) * CHUNK)
 
-        pairs_by_token = pairs[:].rearrange("p (c t) -> p c t", t=2)
-        for piece, (first, width, on_scalar) in zip(pair_pieces, PAIR_LOADS):
-            source = piece[:].rearrange("p t c -> p c t")
-            if on_scalar > 0:
-                nc.scalar.copy(pairs_by_token[:, first : first + on_scalar, :], source[:, 0:on_scalar, :])
-            nc.vector.tensor_copy(pairs_by_token[:, first + on_scalar : first + width, :], source[:, on_scalar:width, :])
-        for c in range(CHUNKS):
-            first_words = woven[c][:].bitcast(U32).rearrange("p (e h) -> p e h", h=2)[:, :, 0]
-            nc.vector.tensor_copy(first_words, pairs[:].bitcast(U32).indirect(entries(c)))
-
-        for first in range(0, T, LAST_ROW_LOAD):
-            cols = slice(first, first + LAST_ROW_LOAD)
-            nc.scalar.copy(row_bf16[3][:, cols], row_f32[3][:, cols])
-        for c in range(CHUNKS):
-            gather_row(3, c)
-
-        halves = CHUNKS // 2
-        x_codes = [keep.tile([P, 2 * CHUNK], U32, name="x_codes%d" % h, align_bytes=64) for h in range(halves)]
-        x_scales = [keep.tile([P, 2 * CHUNK], U8, name="x_scales%d" % h, align_bytes=64) for h in range(halves)]
+        x_codes = [keep.tile([P, CHUNK], U32, name="x_codes%d" % c, align_bytes=64) for c in range(CHUNKS - 1)]
+        x_scales = [keep.tile([P, CHUNK], U8, name="x_scales%d" % c, align_bytes=64) for c in range(CHUNKS)]
         layer_sums = [psum.tile([P, CHUNK], F32, name="layer_sums%d" % c) for c in range(CHUNKS)]
-        gate_sums = [psum.tile([P, 2 * CHUNK], F32, name="gate_sums%d" % h) for h in range(halves)]
-        gate_tanh = [keep.tile([P, 2 * CHUNK], F32, name="gate_tanh%d" % h) for h in range(halves)]
+        gate_sums = [psum.tile([P, CHUNK], F32, name="gate_sums%d" % c) for c in range(CHUNKS)]
+        gate_tanh = [keep.tile([P, CHUNK], F32, name="gate_tanh%d" % c) for c in range(CHUNKS)]
         layer = [keep.tile([P, CHUNK], F32, name="layer%d" % c) for c in range(CHUNKS)]
-        diff = [keep.tile([P, CHUNK], F32, name="diff%d" % c) for c in range(CHUNKS)]
+        diff = [keep.tile([P, CHUNK], F32, name="diff%d" % c, tag="diff%d" % c, align_bytes=64) for c in range(CHUNKS)]
         gated = [keep.tile([P, CHUNK], F32, name="gated%d" % c) for c in range(CHUNKS)]
         result = [keep.tile([P, CHUNK], F32, name="result%d" % c) for c in range(CHUNKS)]
 
-        def within_half(c):
-            return slice((c % 2) * CHUNK, (c % 2 + 1) * CHUNK)
+        def quantise(c):
+            nc.vector.quantize_mx(out=x_codes[c][:].bitcast(FP8X4), scales=x_scales[c][:], in_=woven[:, PACK * c * CHUNK : PACK * (c + 1) * CHUNK])
 
-        def product(sums, i, h, cols):
+        def product(sums, i, c):
             nc.tensor.matmul_mx(
-                out=sums[:],
+                out=sums[c][:],
                 lhsT=w_words[i][:].bitcast(FP4X4),
                 lhsT_scale=w_scales[i][:],
-                rhs=x_codes[h][:, cols].bitcast(FP8X4),
-                rhs_scale=x_scales[h][:, cols],
+                rhs=x_codes[c][:].bitcast(FP8X4),
+                rhs_scale=x_scales[c][:],
                 start=True,
                 stop=True,
             )
 
-        for c in range(CHUNKS):
-            h, cols = c // 2, within_half(c)
-            nc.vector.quantize_mx(out=x_codes[h][:, cols].bitcast(FP8X4), scales=x_scales[h][:, cols], in_=woven[c][:])
-            product(layer_sums[c], 0, h, cols)
-            if c % 2 == 1:
-                product(gate_sums[h], 1, h, slice(0, 2 * CHUNK))
-        for c in range(CHUNKS):
-            nc.scalar.activation(layer[c][:], layer_sums[c][:], ACT.Gelu_apprx_tanh, bias=zero_bias[:])
-            if c % 2 == 1:
-                nc.scalar.activation(gate_tanh[c // 2][:], gate_sums[c // 2][:], ACT.Tanh, scale=0.5)
+        def gelu(c):
+            nc.scalar.activation(layer[c][:], layer_sums[c][:], ACT.Gelu_apprx_tanh)
+
+        def tanh(c, bias=0.0):
+            nc.scalar.activation(gate_tanh[c][:], gate_sums[c][:], ACT.Tanh, scale=0.5, bias=bias)
 
         def subtract(c):
-            nc.vector.tensor_tensor(diff[c][:], res_sb[:].indirect(entries(c)), layer[c][:], ALU.subtract)
+            nc.vector.tensor_tensor(diff[c][:], res_sb[:].indirect(entries(c * CHUNK, (c + 1) * CHUNK)), layer[c][:], ALU.subtract)
 
         def gate(c):
-            a = gate_tanh[c // 2][:, within_half(c)]
-            nc.vector.scalar_tensor_tensor(gated[c][:], a, 1.0, diff[c][:], ALU.subtract, ALU.mult)
+            nc.vector.scalar_tensor_tensor(gated[c][:], gate_tanh[c][:], 1.0, diff[c][:], ALU.subtract, ALU.mult)
 
         def finish(c):
             nc.vector.scalar_tensor_tensor(result[c][:], gated[c][:], -0.5, layer[c][:], ALU.mult, ALU.add)
             nc.sync.dma_start(out=out[:, c * CHUNK : (c + 1) * CHUNK], in_=result[c][:])
 
-        for h in range(halves):
-            for step in (subtract, gate, finish):
-                step(2 * h)
-                step(2 * h + 1)
+        last = CHUNKS - 1
+        for c in range(last):
+            quantise(c)
+            product(layer_sums, 0, c)
+            product(gate_sums, 1, c)
+        gelu(0)
+        gelu(1)
+        tanh(0, tanh_bias)
+        gather_on_scalar(PACK - 1, last * CHUNK, S)
+        tanh(1)
+        gelu(2)
+        tanh(2)
+        subtract(0)
+        subtract(1)
+        gate(0)
+        x_codes.append(keep.tile([P, CHUNK], U32, name="x_codes_last", tag="diff0", align_bytes=64))
+        quantise(last)
+        product(layer_sums, 0, last)
+        product(gate_sums, 1, last)
+        gelu(last)
+        tanh(last)
+        gate(1)
+        finish(0)
+        finish(1)
+        for step in (subtract, gate, finish):
+            step(2)
+            step(3)

@@ -21,8 +21,8 @@ PACK = 4
 LIST_ROWS = 16
 CHUNK = 256
 CHUNKS = S // CHUNK
-ROW_LOADS = ((0, 1536), (1536, 512))
-VECTOR_ENTRIES = (384, 384, CHUNK, CHUNK)
+ROW_LOADS = ((0, 1408), (1408, 640))
+VECTOR_ENTRIES = (384, 352, 384, 384)
 
 
 def tile_picked_highway_gelu_l_kernel(tc, xT, res, w1_words, w1_scales, w2_words, w2_scales, offs, out):
@@ -42,10 +42,10 @@ def tile_picked_highway_gelu_l_kernel(tc, xT, res, w1_words, w1_scales, w2_words
         woven = keep.tile([P, PACK * S], BF16, name="woven", align_bytes=64)
         woven_by_entry = woven[:].rearrange("p (e t) -> p e t", t=PACK)
         zero = keep.tile([P, 1], F32, name="zero")
-        tanh_bias = woven_by_entry[:, S - CHUNK, PACK - 1 : PACK]
+        zero_bias = keep.tile([P, 1], F32, name="zero_bias")
 
         nc.vector.memset(zero[:], 0.0)
-        nc.scalar.activation(tanh_bias, zero[:], ACT.Gelu_apprx_tanh)
+        nc.scalar.activation(zero_bias[:], zero[:], ACT.Gelu_apprx_tanh)
 
         def entries(first, end):
             return offsets[:, first // LIST_ROWS : end // LIST_ROWS]
@@ -62,9 +62,9 @@ def tile_picked_highway_gelu_l_kernel(tc, xT, res, w1_words, w1_scales, w2_words
         load_words(0, w1_words)
         load_words(1, w2_words)
         nc.sync.dma_start(out=res_sb[:], in_=res)
-        for tile, dram in zip(w_scales, (w1_scales, w2_scales)):
+        for tile, dram, queue in zip(w_scales, (w1_scales, w2_scales), (nc.scalar, nc.gpsimd)):
             for q in range(4):
-                nc.gpsimd.dma_start(
+                queue.dma_start(
                     out=tile[32 * q : 32 * q + 4, :].bitcast(I32),
                     in_=dram[0][4 * q : 4 * q + 4, :].bitcast(I32),
                 )
@@ -82,16 +82,17 @@ def tile_picked_highway_gelu_l_kernel(tc, xT, res, w1_words, w1_scales, w2_words
             gather_on_vector(t, 0, VECTOR_ENTRIES[t])
             if t < PACK - 1:
                 gather_on_scalar(t, VECTOR_ENTRIES[t], S)
-        for c in range(1, CHUNKS - 1):
-            gather_on_scalar(PACK - 1, c * CHUNK, (c + 1) * CHUNK)
+            else:
+                gather_on_scalar(t, VECTOR_ENTRIES[t], S - CHUNK)
+                gather_on_scalar(t, S - CHUNK, S)
 
-        x_codes = [keep.tile([P, CHUNK], U32, name="x_codes%d" % c, align_bytes=64) for c in range(CHUNKS - 1)]
+        x_codes = [keep.tile([P, CHUNK], U32, name="x_codes%d" % c, align_bytes=64) for c in range(CHUNKS)]
         x_scales = [keep.tile([P, CHUNK], U8, name="x_scales%d" % c, align_bytes=64) for c in range(CHUNKS)]
         layer_sums = [psum.tile([P, CHUNK], F32, name="layer_sums%d" % c) for c in range(CHUNKS)]
         gate_sums = [psum.tile([P, CHUNK], F32, name="gate_sums%d" % c) for c in range(CHUNKS)]
         gate_tanh = [keep.tile([P, CHUNK], F32, name="gate_tanh%d" % c) for c in range(CHUNKS)]
         layer = [keep.tile([P, CHUNK], F32, name="layer%d" % c) for c in range(CHUNKS)]
-        diff = [keep.tile([P, CHUNK], F32, name="diff%d" % c, tag="diff%d" % c, align_bytes=64) for c in range(CHUNKS)]
+        diff = [keep.tile([P, CHUNK], F32, name="diff%d" % c) for c in range(CHUNKS)]
         gated = [keep.tile([P, CHUNK], F32, name="gated%d" % c) for c in range(CHUNKS)]
         result = [keep.tile([P, CHUNK], F32, name="result%d" % c) for c in range(CHUNKS)]
 
@@ -110,10 +111,10 @@ def tile_picked_highway_gelu_l_kernel(tc, xT, res, w1_words, w1_scales, w2_words
             )
 
         def gelu(c):
-            nc.scalar.activation(layer[c][:], layer_sums[c][:], ACT.Gelu_apprx_tanh)
+            nc.scalar.activation(layer[c][:], layer_sums[c][:], ACT.Gelu_apprx_tanh, bias=zero_bias[:])
 
-        def tanh(c, bias=0.0):
-            nc.scalar.activation(gate_tanh[c][:], gate_sums[c][:], ACT.Tanh, scale=0.5, bias=bias)
+        def tanh(c):
+            nc.scalar.activation(gate_tanh[c][:], gate_sums[c][:], ACT.Tanh, scale=0.5)
 
         def subtract(c):
             nc.vector.tensor_tensor(diff[c][:], res_sb[:].indirect(entries(c * CHUNK, (c + 1) * CHUNK)), layer[c][:], ALU.subtract)
@@ -125,30 +126,11 @@ def tile_picked_highway_gelu_l_kernel(tc, xT, res, w1_words, w1_scales, w2_words
             nc.vector.scalar_tensor_tensor(result[c][:], gated[c][:], -0.5, layer[c][:], ALU.mult, ALU.add)
             nc.sync.dma_start(out=out[:, c * CHUNK : (c + 1) * CHUNK], in_=result[c][:])
 
-        last = CHUNKS - 1
-        for c in range(last):
+        for c in range(CHUNKS):
             quantise(c)
             product(layer_sums, 0, c)
             product(gate_sums, 1, c)
-        gelu(0)
-        gelu(1)
-        tanh(0, tanh_bias)
-        gather_on_scalar(PACK - 1, last * CHUNK, S)
-        tanh(1)
-        gelu(2)
-        tanh(2)
-        subtract(0)
-        subtract(1)
-        gate(0)
-        x_codes.append(keep.tile([P, CHUNK], U32, name="x_codes_last", tag="diff0", align_bytes=64))
-        quantise(last)
-        product(layer_sums, 0, last)
-        product(gate_sums, 1, last)
-        gelu(last)
-        tanh(last)
-        gate(1)
-        finish(0)
-        finish(1)
-        for step in (subtract, gate, finish):
-            step(2)
-            step(3)
+        for pair in ((0, 1), (2, 3)):
+            for step in (gelu, tanh, subtract, gate, finish):
+                for c in pair:
+                    step(c)

@@ -1,6 +1,7 @@
 from contextlib import ExitStack
 
 import concourse.mybir as mybir
+from concourse.masks import make_identity
 
 K, T, S, N = 512, 2048, 1024, 128
 FLOPS = 2 * 2 * K * S * N
@@ -22,7 +23,7 @@ LIST_ROWS = 16
 CHUNK = 256
 CHUNKS = S // CHUNK
 ROW_LOADS = ((0, 1408), (1408, 640))
-VECTOR_ENTRIES = (384, 352, 384, 384)
+VECTOR_ENTRIES = (352, 352, 352, 352)
 
 
 def tile_picked_highway_gelu_l_kernel(tc, xT, res, w1_words, w1_scales, w2_words, w2_scales, offs, out):
@@ -43,6 +44,8 @@ def tile_picked_highway_gelu_l_kernel(tc, xT, res, w1_words, w1_scales, w2_words
         woven_by_entry = woven[:].rearrange("p (e t) -> p e t", t=PACK)
         zero = keep.tile([P, 1], F32, name="zero")
         zero_bias = keep.tile([P, 1], F32, name="zero_bias")
+        identity = keep.tile([P, P], F32, name="identity")
+        make_identity(nc, identity[:])
 
         nc.vector.memset(zero[:], 0.0)
         nc.scalar.activation(zero_bias[:], zero[:], ACT.Gelu_apprx_tanh)
@@ -88,8 +91,8 @@ def tile_picked_highway_gelu_l_kernel(tc, xT, res, w1_words, w1_scales, w2_words
 
         x_codes = [keep.tile([P, CHUNK], U32, name="x_codes%d" % c, align_bytes=64) for c in range(CHUNKS)]
         x_scales = [keep.tile([P, CHUNK], U8, name="x_scales%d" % c, align_bytes=64) for c in range(CHUNKS)]
-        layer_sums = [psum.tile([P, CHUNK], F32, name="layer_sums%d" % c) for c in range(CHUNKS)]
-        gate_sums = [psum.tile([P, CHUNK], F32, name="gate_sums%d" % c) for c in range(CHUNKS)]
+        layer_sums = [psum.tile([P, CHUNK], F32, name="layer_sums%d" % c, tag="layer%d" % c) for c in range(CHUNKS)]
+        gate_sums = [psum.tile([P, CHUNK], F32, name="gate_sums%d" % c, tag="gate%d" % c) for c in range(CHUNKS)]
         gate_tanh = [keep.tile([P, CHUNK], F32, name="gate_tanh%d" % c) for c in range(CHUNKS)]
         layer = [keep.tile([P, CHUNK], F32, name="layer%d" % c) for c in range(CHUNKS)]
         diff = [keep.tile([P, CHUNK], F32, name="diff%d" % c) for c in range(CHUNKS)]
@@ -114,23 +117,72 @@ def tile_picked_highway_gelu_l_kernel(tc, xT, res, w1_words, w1_scales, w2_words
             nc.scalar.activation(layer[c][:], layer_sums[c][:], ACT.Gelu_apprx_tanh, bias=zero_bias[:])
 
         def tanh(c):
-            nc.scalar.activation(gate_tanh[c][:], gate_sums[c][:], ACT.Tanh, scale=0.5)
+            nc.scalar.activation(gate_tanh[c][:], gate_sums[c][:], ACT.Tanh, scale=-0.5)
 
         def subtract(c):
             nc.vector.tensor_tensor(diff[c][:], res_sb[:].indirect(entries(c * CHUNK, (c + 1) * CHUNK)), layer[c][:], ALU.subtract)
 
         def gate(c):
-            nc.vector.scalar_tensor_tensor(gated[c][:], gate_tanh[c][:], 1.0, diff[c][:], ALU.subtract, ALU.mult)
+            nc.vector.scalar_tensor_tensor(gated[c][:], gate_tanh[c][:], 1.0, diff[c][:], ALU.add, ALU.mult)
+
+        def store(c):
+            nc.sync.dma_start(out=out[:, c * CHUNK : (c + 1) * CHUNK], in_=result[c][:])
 
         def finish(c):
-            nc.vector.scalar_tensor_tensor(result[c][:], gated[c][:], -0.5, layer[c][:], ALU.mult, ALU.add)
-            nc.sync.dma_start(out=out[:, c * CHUNK : (c + 1) * CHUNK], in_=result[c][:])
+            nc.vector.scalar_tensor_tensor(result[c][:], gated[c][:], 0.5, layer[c][:], ALU.mult, ALU.add)
+            store(c)
 
         for c in range(CHUNKS):
             quantise(c)
             product(layer_sums, 0, c)
             product(gate_sums, 1, c)
-        for pair in ((0, 1), (2, 3)):
-            for step in (gelu, tanh, subtract, gate, finish):
-                for c in pair:
-                    step(c)
+        def turn(sums, source, start, stop):
+            nc.tensor.matmul(sums, lhsT=source, rhs=identity[:], start=start, stop=stop, is_transpose=True)
+
+        blocks = [slice(b * P, (b + 1) * P) for b in range(CHUNK // P)]
+
+        def open_sums(c):
+            banks = [psum.tile([P, P], F32, name="turned_sums%d_%d" % (c, b), tag="layer%d" % (2 * c + b)) for b in range(len(blocks))]
+            for sums, cols in zip(banks, blocks):
+                turn(sums[:], layer[c][:, cols], True, False)
+                turn(sums[:], layer[c][:, cols], False, False)
+            return banks
+
+        def close_sums(c, banks):
+            for sums, cols in zip(banks, blocks):
+                turn(sums[:], gated[c][:, cols], False, True)
+
+        def turn_back(c, banks):
+            turned = keep.tile([P, CHUNK], F32, name="turned%d" % c)
+            for sums, cols in zip(banks, blocks):
+                nc.scalar.activation(turned[:, cols], sums[:], ACT.Copy, scale=0.5)
+            result_sums = psum.tile([P, CHUNK], F32, name="result_sums%d" % c, tag="gate%d" % c)
+            for cols in blocks:
+                turn(result_sums[:, cols], turned[:, cols], True, True)
+            return result_sums
+
+        def copy_out(c, result_sums):
+            nc.scalar.copy(result[c][:], result_sums[:])
+            store(c)
+
+        for step in (gelu, tanh):
+            step(0)
+            step(1)
+        banks0 = open_sums(0)
+        gelu(2)
+        gelu(3)
+        banks1 = open_sums(1)
+        for step in (subtract, gate):
+            step(0)
+            step(1)
+        close_sums(0, banks0)
+        close_sums(1, banks1)
+        tanh(2)
+        sums0 = turn_back(0, banks0)
+        tanh(3)
+        sums1 = turn_back(1, banks1)
+        copy_out(0, sums0)
+        copy_out(1, sums1)
+        for step in (subtract, gate, finish):
+            step(2)
+            step(3)

@@ -23,7 +23,8 @@ LIST_ROWS = 16
 CHUNK = 256
 CHUNKS = S // CHUNK
 ROW_LOADS = ((0, 1408), (1408, 640))
-VECTOR_ENTRIES = (352, 352, 352, 352)
+VECTOR_ENTRIES = (352, 352, 384, 384)
+TURNED_BLOCKS = 3
 
 
 def tile_picked_highway_gelu_l_kernel(tc, xT, res, w1_words, w1_scales, w2_words, w2_scales, offs, out):
@@ -93,11 +94,18 @@ def tile_picked_highway_gelu_l_kernel(tc, xT, res, w1_words, w1_scales, w2_words
         x_scales = [keep.tile([P, CHUNK], U8, name="x_scales%d" % c, align_bytes=64) for c in range(CHUNKS)]
         layer_sums = [psum.tile([P, CHUNK], F32, name="layer_sums%d" % c, tag="layer%d" % c) for c in range(CHUNKS)]
         gate_sums = [psum.tile([P, CHUNK], F32, name="gate_sums%d" % c, tag="gate%d" % c) for c in range(CHUNKS)]
-        gate_tanh = [keep.tile([P, CHUNK], F32, name="gate_tanh%d" % c) for c in range(CHUNKS)]
-        layer = [keep.tile([P, CHUNK], F32, name="layer%d" % c) for c in range(CHUNKS)]
-        diff = [keep.tile([P, CHUNK], F32, name="diff%d" % c) for c in range(CHUNKS)]
-        gated = [keep.tile([P, CHUNK], F32, name="gated%d" % c) for c in range(CHUNKS)]
-        result = [keep.tile([P, CHUNK], F32, name="result%d" % c) for c in range(CHUNKS)]
+        gate_tanh = keep.tile([P, S], F32, name="gate_tanh")
+        layer = keep.tile([P, S], F32, name="layer")
+        diff = keep.tile([P, S], F32, name="diff")
+        gated = keep.tile([P, S], F32, name="gated")
+        turned = keep.tile([P, TURNED_BLOCKS * P], F32, name="turned")
+        result = keep.tile([P, S], F32, name="result")
+
+        def chunk(c):
+            return slice(c * CHUNK, (c + 1) * CHUNK)
+
+        def block(b):
+            return slice(b * P, (b + 1) * P)
 
         def quantise(c):
             nc.vector.quantize_mx(out=x_codes[c][:].bitcast(FP8X4), scales=x_scales[c][:], in_=woven[:, PACK * c * CHUNK : PACK * (c + 1) * CHUNK])
@@ -114,75 +122,56 @@ def tile_picked_highway_gelu_l_kernel(tc, xT, res, w1_words, w1_scales, w2_words
             )
 
         def gelu(c):
-            nc.scalar.activation(layer[c][:], layer_sums[c][:], ACT.Gelu_apprx_tanh, bias=zero_bias[:])
+            nc.scalar.activation(layer[:, chunk(c)], layer_sums[c][:], ACT.Gelu_apprx_tanh, bias=zero_bias[:])
 
         def tanh(c):
-            nc.scalar.activation(gate_tanh[c][:], gate_sums[c][:], ACT.Tanh, scale=-0.5)
+            nc.scalar.activation(gate_tanh[:, chunk(c)], gate_sums[c][:], ACT.Tanh, scale=-0.5)
 
         def subtract(c):
-            nc.vector.tensor_tensor(diff[c][:], res_sb[:].indirect(entries(c * CHUNK, (c + 1) * CHUNK)), layer[c][:], ALU.subtract)
+            cols = chunk(c)
+            nc.vector.tensor_tensor(diff[:, cols], res_sb[:].indirect(entries(cols.start, cols.stop)), layer[:, cols], ALU.subtract)
 
         def gate(c):
-            nc.vector.scalar_tensor_tensor(gated[c][:], gate_tanh[c][:], 1.0, diff[c][:], ALU.add, ALU.mult)
+            cols = chunk(c)
+            nc.vector.scalar_tensor_tensor(gated[:, cols], gate_tanh[:, cols], 1.0, diff[:, cols], ALU.add, ALU.mult)
 
-        def store(c):
-            nc.sync.dma_start(out=out[:, c * CHUNK : (c + 1) * CHUNK], in_=result[c][:])
+        def finish(cols):
+            nc.vector.scalar_tensor_tensor(result[:, cols], gated[:, cols], 0.5, layer[:, cols], ALU.mult, ALU.add)
+            nc.sync.dma_start(out=out[:, cols], in_=result[:, cols])
 
-        def finish(c):
-            nc.vector.scalar_tensor_tensor(result[c][:], gated[c][:], 0.5, layer[c][:], ALU.mult, ALU.add)
-            store(c)
+        def turn(sums, source, start, stop):
+            nc.tensor.matmul(sums, lhsT=source, rhs=identity[:], start=start, stop=stop, is_transpose=True)
 
         for c in range(CHUNKS):
             quantise(c)
             product(layer_sums, 0, c)
             product(gate_sums, 1, c)
-        def turn(sums, source, start, stop):
-            nc.tensor.matmul(sums, lhsT=source, rhs=identity[:], start=start, stop=stop, is_transpose=True)
+        for pair in ((0, 1), (2, 3)):
+            for step in (gelu, tanh):
+                for c in pair:
+                    step(c)
 
-        blocks = [slice(b * P, (b + 1) * P) for b in range(CHUNK // P)]
-
-        def open_sums(c):
-            banks = [psum.tile([P, P], F32, name="turned_sums%d_%d" % (c, b), tag="layer%d" % (2 * c + b)) for b in range(len(blocks))]
-            for sums, cols in zip(banks, blocks):
-                turn(sums[:], layer[c][:, cols], True, False)
-                turn(sums[:], layer[c][:, cols], False, False)
-            return banks
-
-        def close_sums(c, banks):
-            for sums, cols in zip(banks, blocks):
-                turn(sums[:], gated[c][:, cols], False, True)
-
-        def turn_back(c, banks):
-            turned = keep.tile([P, CHUNK], F32, name="turned%d" % c)
-            for sums, cols in zip(banks, blocks):
-                nc.scalar.activation(turned[:, cols], sums[:], ACT.Copy, scale=0.5)
-            result_sums = psum.tile([P, CHUNK], F32, name="result_sums%d" % c, tag="gate%d" % c)
-            for cols in blocks:
-                turn(result_sums[:, cols], turned[:, cols], True, True)
-            return result_sums
-
-        def copy_out(c, result_sums):
-            nc.scalar.copy(result[c][:], result_sums[:])
-            store(c)
-
-        for step in (gelu, tanh):
-            step(0)
-            step(1)
-        banks0 = open_sums(0)
-        gelu(2)
-        gelu(3)
-        banks1 = open_sums(1)
+        turned_sums = [psum.tile([P, P], F32, name="turned_sums%d" % b, tag="layer%d" % b) for b in range(TURNED_BLOCKS)]
+        for b in range(TURNED_BLOCKS):
+            turn(turned_sums[b][:], layer[:, block(b)], True, False)
+            turn(turned_sums[b][:], layer[:, block(b)], False, False)
         for step in (subtract, gate):
             step(0)
             step(1)
-        close_sums(0, banks0)
-        close_sums(1, banks1)
-        tanh(2)
-        sums0 = turn_back(0, banks0)
-        tanh(3)
-        sums1 = turn_back(1, banks1)
-        copy_out(0, sums0)
-        copy_out(1, sums1)
-        for step in (subtract, gate, finish):
-            step(2)
-            step(3)
+        for b in range(TURNED_BLOCKS):
+            turn(turned_sums[b][:], gated[:, block(b)], False, True)
+            nc.scalar.activation(turned[:, block(b)], turned_sums[b][:], ACT.Copy, scale=0.5)
+        for c in range(2):
+            first, end = c * CHUNK, min((c + 1) * CHUNK, TURNED_BLOCKS * P)
+            result_sums = psum.tile([P, end - first], F32, name="result_sums%d" % c, tag="gate%d" % c)
+            for b in range(first // P, end // P):
+                turn(result_sums[:, b * P - first : (b + 1) * P - first], turned[:, block(b)], True, True)
+            nc.scalar.copy(result[:, first:end], result_sums[:])
+            nc.scalar.dma_start(out=out[:, first:end], in_=result[:, first:end])
+        subtract(2)
+        finish(slice(TURNED_BLOCKS * P, 2 * CHUNK))
+        subtract(3)
+        gate(2)
+        gate(3)
+        finish(chunk(2))
+        finish(chunk(3))

@@ -23,7 +23,7 @@ LIST_ROWS = 16
 CHUNK = 256
 CHUNKS = S // CHUNK
 ROW_LOADS = ((0, 1408), (1408, 640))
-VECTOR_ENTRIES = (352, 352, 384, 384)
+VECTOR_ENTRIES = (352, 352, 352, 352)
 TURNED_BLOCKS = 3
 
 

@@ -22,8 +22,8 @@ PACK = 4
 LIST_ROWS = 16
 CHUNK = 256
 CHUNKS = S // CHUNK
-ROW_LOADS = ((0, 1408), (1408, 640))
-VECTOR_ENTRIES = (352, 352, 352, 352)
+ROW_CUTS = (1664, 1408, 1408, 1408)
+VECTOR_ENTRIES = (384, 352, 352, 352)
 TURNED_BLOCKS = 3
 
 
@@ -57,11 +57,13 @@ def tile_picked_highway_gelu_l_kernel(tc, xT, res, w1_words, w1_scales, w2_words
         def load_words(i, dram):
             nc.sync.dma_start(out=w_words[i][:].bitcast(I32), in_=dram[0].bitcast(I32))
 
+        def pieces(t):
+            return slice(0, ROW_CUTS[t]), slice(ROW_CUTS[t], T)
+
         for t in range(PACK):
-            for first, width in ROW_LOADS:
-                cols = slice(first, first + width)
+            for cols in pieces(t):
                 nc.sync.dma_start(out=row_f32[t][:, cols], in_=x_rows[:, t, cols])
-                if t == 0 and first == 0:
+                if t == 0 and cols.start == 0:
                     nc.sync.dma_start(offsets[:], offs)
         load_words(0, w1_words)
         load_words(1, w2_words)
@@ -80,8 +82,11 @@ def tile_picked_highway_gelu_l_kernel(tc, xT, res, w1_words, w1_scales, w2_words
             nc.scalar.activation(woven_by_entry[:, first:end, t], row_bf16[t][:].indirect(entries(first, end)), ACT.Copy)
 
         for t in range(PACK):
-            for first, width in ROW_LOADS:
-                cols = slice(first, first + width)
+            for cols in pieces(t):
+                if t == 0:
+                    cut = cols.stop - (cols.stop - cols.start) // 3 // 16 * 16
+                    nc.scalar.copy(row_bf16[t][:, cut : cols.stop], row_f32[t][:, cut : cols.stop])
+                    cols = slice(cols.start, cut)
                 nc.vector.tensor_copy(row_bf16[t][:, cols], row_f32[t][:, cols])
             gather_on_vector(t, 0, VECTOR_ENTRIES[t])
             if t < PACK - 1:

@@ -22,8 +22,8 @@ PACK = 4
 LIST_ROWS = 16
 CHUNK = 256
 CHUNKS = S // CHUNK
-ROW_CUTS = (1664, 1408, 1408, 1408)
-VECTOR_ENTRIES = (384, 352, 352, 352)
+ROW_CUTS = ((0, 1664, T), (0, 960, T), (0, 960, T), (0, 768, 1664, T))
+VECTOR_ENTRIES = (448, 448, 384, 352)
 TURNED_BLOCKS = 3
 
 
@@ -58,19 +58,19 @@ def tile_picked_highway_gelu_l_kernel(tc, xT, res, w1_words, w1_scales, w2_words
             nc.sync.dma_start(out=w_words[i][:].bitcast(I32), in_=dram[0].bitcast(I32))
 
         def pieces(t):
-            return slice(0, ROW_CUTS[t]), slice(ROW_CUTS[t], T)
+            return [slice(first, end) for first, end in zip(ROW_CUTS[t], ROW_CUTS[t][1:])]
 
         for t in range(PACK):
             for cols in pieces(t):
                 nc.sync.dma_start(out=row_f32[t][:, cols], in_=x_rows[:, t, cols])
-                if t == 0 and cols.start == 0:
-                    nc.sync.dma_start(offsets[:], offs)
+            if t == 0:
+                nc.sync.dma_start(offsets[:], offs)
         load_words(0, w1_words)
         load_words(1, w2_words)
         nc.sync.dma_start(out=res_sb[:], in_=res)
         for tile, dram, queue in zip(w_scales, (w1_scales, w2_scales), (nc.scalar, nc.gpsimd)):
             for q in range(4):
-                queue.dma_start(
+                (queue if q < 2 else nc.scalar).dma_start(
                     out=tile[32 * q : 32 * q + 4, :].bitcast(I32),
                     in_=dram[0][4 * q : 4 * q + 4, :].bitcast(I32),
                 )
@@ -87,7 +87,10 @@ def tile_picked_highway_gelu_l_kernel(tc, xT, res, w1_words, w1_scales, w2_words
                     cut = cols.stop - (cols.stop - cols.start) // 3 // 16 * 16
                     nc.scalar.copy(row_bf16[t][:, cut : cols.stop], row_f32[t][:, cut : cols.stop])
                     cols = slice(cols.start, cut)
-                nc.vector.tensor_copy(row_bf16[t][:, cols], row_f32[t][:, cols])
+                if t > 0 and cols.start == 0:
+                    nc.gpsimd.tensor_scalar(row_bf16[t][:, cols], row_f32[t][:, cols], 1.0, 0.0, ALU.mult, ALU.add)
+                else:
+                    nc.vector.tensor_copy(row_bf16[t][:, cols], row_f32[t][:, cols])
             gather_on_vector(t, 0, VECTOR_ENTRIES[t])
             if t < PACK - 1:
                 gather_on_scalar(t, VECTOR_ENTRIES[t], S)

@@ -22,8 +22,7 @@ PACK = 4
 LIST_ROWS = 16
 CHUNK = 256
 CHUNKS = S // CHUNK
-ROW_CUTS = ((0, 1664, T), (0, 960, T), (0, 960, T), (0, 768, 1664, T))
-VECTOR_ENTRIES = (448, 448, 384, 352)
+VECTOR_ENTRIES = (256, 256, 512, 256)
 TURNED_BLOCKS = 3
 
 
@@ -39,64 +38,51 @@ def tile_picked_highway_gelu_l_kernel(tc, xT, res, w1_words, w1_scales, w2_words
         res_sb = keep.tile([P, T], F32, name="res_sb")
         w_words = [keep.tile([P, 2 * N], U8, name="w_words%d" % i, align_bytes=64) for i in range(2)]
         w_scales = [keep.tile([P, N], U8, name="w_scales%d" % i, align_bytes=64) for i in range(2)]
-        row_f32 = [keep.tile([P, T], F32, name="row_f32_%d" % t) for t in range(PACK)]
-        row_bf16 = [keep.tile([P, T], BF16, name="row_bf16_%d" % t) for t in range(PACK)]
-        woven = keep.tile([P, PACK * S], BF16, name="woven", align_bytes=64)
-        woven_by_entry = woven[:].rearrange("p (e t) -> p e t", t=PACK)
+        rows = [keep.tile([P, T], F32, name="row%d" % t) for t in range(PACK)]
+        low_pair = keep.tile([P, 2, S - CHUNK], BF16, name="low_pair")
+        high_pair = {c: keep.tile([P, 2, CHUNK], BF16, name="high_pair%d" % c) for c in range(1, CHUNKS)}
+        woven = [keep.tile([P, CHUNK, PACK], BF16, name="woven%d" % c, align_bytes=64) for c in range(CHUNKS)]
         zero = keep.tile([P, 1], F32, name="zero")
         zero_bias = keep.tile([P, 1], F32, name="zero_bias")
         identity = keep.tile([P, P], F32, name="identity")
-        make_identity(nc, identity[:])
 
         nc.vector.memset(zero[:], 0.0)
         nc.scalar.activation(zero_bias[:], zero[:], ACT.Gelu_apprx_tanh)
 
-        def entries(first, end):
-            return offsets[:, first // LIST_ROWS : end // LIST_ROWS]
-
-        def load_words(i, dram):
-            nc.sync.dma_start(out=w_words[i][:].bitcast(I32), in_=dram[0].bitcast(I32))
-
-        def pieces(t):
-            return [slice(first, end) for first, end in zip(ROW_CUTS[t], ROW_CUTS[t][1:])]
-
-        for t in range(PACK):
-            for cols in pieces(t):
-                nc.sync.dma_start(out=row_f32[t][:, cols], in_=x_rows[:, t, cols])
-            if t == 0:
-                nc.sync.dma_start(offsets[:], offs)
-        load_words(0, w1_words)
-        load_words(1, w2_words)
-        nc.sync.dma_start(out=res_sb[:], in_=res)
-        for tile, dram, queue in zip(w_scales, (w1_scales, w2_scales), (nc.scalar, nc.gpsimd)):
+        def load_scales(queue, i, dram):
             for q in range(4):
-                (queue if q < 2 else nc.scalar).dma_start(
-                    out=tile[32 * q : 32 * q + 4, :].bitcast(I32),
+                queue.dma_start(
+                    out=w_scales[i][32 * q : 32 * q + 4, :].bitcast(I32),
                     in_=dram[0][4 * q : 4 * q + 4, :].bitcast(I32),
                 )
 
-        def gather_on_vector(t, first, end):
-            nc.vector.tensor_copy(woven_by_entry[:, first:end, t], row_f32[t][:].indirect(entries(first, end)))
-
-        def gather_on_scalar(t, first, end):
-            nc.scalar.activation(woven_by_entry[:, first:end, t], row_bf16[t][:].indirect(entries(first, end)), ACT.Copy)
-
         for t in range(PACK):
-            for cols in pieces(t):
-                if t == 0:
-                    cut = cols.stop - (cols.stop - cols.start) // 3 // 16 * 16
-                    nc.scalar.copy(row_bf16[t][:, cut : cols.stop], row_f32[t][:, cut : cols.stop])
-                    cols = slice(cols.start, cut)
-                if t > 0 and cols.start == 0:
-                    nc.gpsimd.tensor_scalar(row_bf16[t][:, cols], row_f32[t][:, cols], 1.0, 0.0, ALU.mult, ALU.add)
-                else:
-                    nc.vector.tensor_copy(row_bf16[t][:, cols], row_f32[t][:, cols])
-            gather_on_vector(t, 0, VECTOR_ENTRIES[t])
-            if t < PACK - 1:
-                gather_on_scalar(t, VECTOR_ENTRIES[t], S)
-            else:
-                gather_on_scalar(t, VECTOR_ENTRIES[t], S - CHUNK)
-                gather_on_scalar(t, S - CHUNK, S)
+            nc.sync.dma_start(out=rows[t][:], in_=x_rows[:, t, :])
+            if t == 0:
+                nc.sync.dma_start(offsets[:], offs)
+                load_scales(nc.sync, 0, w1_scales)
+            if t == 2:
+                load_scales(nc.sync, 1, w2_scales)
+        for tile, dram in zip(w_words, (w1_words, w2_words)):
+            nc.sync.dma_start(out=tile[:].bitcast(I32), in_=dram[0].bitcast(I32))
+        nc.sync.dma_start(out=res_sb[:], in_=res)
+        make_identity(nc, identity[:])
+
+        def entries(first, end):
+            return offsets[:, first // LIST_ROWS : end // LIST_ROWS]
+
+        def chunk(c):
+            return slice(c * CHUNK, (c + 1) * CHUNK)
+
+        def gather(t, plane, base, first, end):
+            cut = min(max(VECTOR_ENTRIES[t], first), end)
+            if first < cut:
+                nc.vector.tensor_copy(plane[:, first - base : cut - base], rows[t][:].indirect(entries(first, cut)))
+            if cut < end:
+                nc.scalar.activation(plane[:, cut - base : end - base], rows[t][:].indirect(entries(cut, end)), ACT.Copy)
+
+        def place(c, half, pair):
+            nc.vector.tensor_copy(woven[c][:, :, 2 * half : 2 * half + 2], pair.rearrange("p t e -> p e t"))
 
         x_codes = [keep.tile([P, CHUNK], U32, name="x_codes%d" % c, align_bytes=64) for c in range(CHUNKS)]
         x_scales = [keep.tile([P, CHUNK], U8, name="x_scales%d" % c, align_bytes=64) for c in range(CHUNKS)]
@@ -109,14 +95,11 @@ def tile_picked_highway_gelu_l_kernel(tc, xT, res, w1_words, w1_scales, w2_words
         turned = keep.tile([P, TURNED_BLOCKS * P], F32, name="turned")
         result = keep.tile([P, S], F32, name="result")
 
-        def chunk(c):
-            return slice(c * CHUNK, (c + 1) * CHUNK)
-
         def block(b):
             return slice(b * P, (b + 1) * P)
 
         def quantise(c):
-            nc.vector.quantize_mx(out=x_codes[c][:].bitcast(FP8X4), scales=x_scales[c][:], in_=woven[:, PACK * c * CHUNK : PACK * (c + 1) * CHUNK])
+            nc.vector.quantize_mx(out=x_codes[c][:].bitcast(FP8X4), scales=x_scales[c][:], in_=woven[c][:].rearrange("p e t -> p (e t)"))
 
         def product(sums, i, c):
             nc.tensor.matmul_mx(
@@ -150,7 +133,18 @@ def tile_picked_highway_gelu_l_kernel(tc, xT, res, w1_words, w1_scales, w2_words
         def turn(sums, source, start, stop):
             nc.tensor.matmul(sums, lhsT=source, rhs=identity[:], start=start, stop=stop, is_transpose=True)
 
+        for t in range(2):
+            gather(t, woven[0][:, :, t], 0, 0, CHUNK)
+            gather(t, low_pair[:, t, :], CHUNK, CHUNK, S)
+        for c in range(1, CHUNKS):
+            place(c, 0, low_pair[:, :, chunk(c - 1)])
+        for t in range(2, PACK):
+            gather(t, woven[0][:, :, t], 0, 0, CHUNK)
+            for c in range(1, CHUNKS):
+                gather(t, high_pair[c][:, t - 2, :], c * CHUNK, c * CHUNK, (c + 1) * CHUNK)
         for c in range(CHUNKS):
+            if c > 0:
+                place(c, 1, high_pair[c][:])
             quantise(c)
             product(layer_sums, 0, c)
             product(gate_sums, 1, c)

@@ -113,7 +113,7 @@ def tile_picked_highway_gelu_l_kernel(tc, xT, res, w1_words, w1_scales, w2_words
             )
 
         def gelu(c):
-            nc.scalar.activation(layer[:, chunk(c)], layer_sums[c][:], ACT.Gelu_apprx_tanh, bias=zero_bias[:])
+            nc.scalar.activation(layer[:, chunk(c)], layer_sums[c][:], ACT.Gelu_apprx_tanh, bias=zero_bias[:] if c == 0 else 0.0)
 
         def tanh(c):
             nc.scalar.activation(gate_tanh[:, chunk(c)], gate_sums[c][:], ACT.Tanh, scale=-0.5)
@@ -140,10 +140,11 @@ def tile_picked_highway_gelu_l_kernel(tc, xT, res, w1_words, w1_scales, w2_words
             place(c, 0, low_pair[:, :, chunk(c - 1)])
         for t in range(2, PACK):
             gather(t, woven[0][:, :, t], 0, 0, CHUNK)
-            for c in range(1, CHUNKS):
+            for c in (1, 3, 2):
                 gather(t, high_pair[c][:, t - 2, :], c * CHUNK, c * CHUNK, (c + 1) * CHUNK)
+        nc.scalar.copy(woven[3][:, :, 2:4], high_pair[3][:].rearrange("p t e -> p e t"))
         for c in range(CHUNKS):
-            if c > 0:
+            if 0 < c < 3:
                 place(c, 1, high_pair[c][:])
             quantise(c)
             product(layer_sums, 0, c)

@@ -22,7 +22,8 @@ PACK = 4
 LIST_ROWS = 16
 CHUNK = 256
 CHUNKS = S // CHUNK
-VECTOR_ENTRIES = (256, 256, 512, 256)
+DIRECT = 384
+PARTS = ((384, 512, "gpsimd"), (512, 640, "gpsimd"), (768, 1024, "scalar"), (640, 768, "vector"))
 TURNED_BLOCKS = 3
 
 
@@ -39,9 +40,9 @@ def tile_picked_highway_gelu_l_kernel(tc, xT, res, w1_words, w1_scales, w2_words
         w_words = [keep.tile([P, 2 * N], U8, name="w_words%d" % i, align_bytes=64) for i in range(2)]
         w_scales = [keep.tile([P, N], U8, name="w_scales%d" % i, align_bytes=64) for i in range(2)]
         rows = [keep.tile([P, T], F32, name="row%d" % t) for t in range(PACK)]
-        low_pair = keep.tile([P, 2, S - CHUNK], BF16, name="low_pair")
-        high_pair = {c: keep.tile([P, 2, CHUNK], BF16, name="high_pair%d" % c) for c in range(1, CHUNKS)}
-        woven = [keep.tile([P, CHUNK, PACK], BF16, name="woven%d" % c, align_bytes=64) for c in range(CHUNKS)]
+        low_pair = keep.tile([P, 2, S - DIRECT], BF16, name="low_pair")
+        high_pair = [keep.tile([P, 2, end - first], BF16, name="high_pair%d" % first) for first, end, engine in PARTS]
+        woven = keep.tile([P, S, PACK], BF16, name="woven", align_bytes=64)
         zero = keep.tile([P, 1], F32, name="zero")
         zero_bias = keep.tile([P, 1], F32, name="zero_bias")
         identity = keep.tile([P, P], F32, name="identity")
@@ -74,15 +75,20 @@ def tile_picked_highway_gelu_l_kernel(tc, xT, res, w1_words, w1_scales, w2_words
         def chunk(c):
             return slice(c * CHUNK, (c + 1) * CHUNK)
 
-        def gather(t, plane, base, first, end):
-            cut = min(max(VECTOR_ENTRIES[t], first), end)
-            if first < cut:
-                nc.vector.tensor_copy(plane[:, first - base : cut - base], rows[t][:].indirect(entries(first, cut)))
-            if cut < end:
-                nc.scalar.activation(plane[:, cut - base : end - base], rows[t][:].indirect(entries(cut, end)), ACT.Copy)
+        def gather_direct(t):
+            nc.vector.tensor_copy(woven[:, :DIRECT, t], rows[t][:].indirect(entries(0, DIRECT)))
 
-        def place(c, half, pair):
-            nc.vector.tensor_copy(woven[c][:, :, 2 * half : 2 * half + 2], pair.rearrange("p t e -> p e t"))
+        def gather(t, plane, first, end):
+            nc.scalar.activation(plane, rows[t][:].indirect(entries(first, end)), ACT.Copy)
+
+        def place(engine, first, end, half, pair):
+            target, source = woven[:, first:end, 2 * half : 2 * half + 2], pair.rearrange("p t e -> p e t")
+            if engine == "gpsimd":
+                nc.gpsimd.tensor_scalar(target, source, 1.0, 0.0, ALU.mult, ALU.add)
+            elif engine == "scalar":
+                nc.scalar.copy(target, source)
+            else:
+                nc.vector.tensor_copy(target, source)
 
         x_codes = [keep.tile([P, CHUNK], U32, name="x_codes%d" % c, align_bytes=64) for c in range(CHUNKS)]
         x_scales = [keep.tile([P, CHUNK], U8, name="x_scales%d" % c, align_bytes=64) for c in range(CHUNKS)]
@@ -99,7 +105,7 @@ def tile_picked_highway_gelu_l_kernel(tc, xT, res, w1_words, w1_scales, w2_words
             return slice(b * P, (b + 1) * P)
 
         def quantise(c):
-            nc.vector.quantize_mx(out=x_codes[c][:].bitcast(FP8X4), scales=x_scales[c][:], in_=woven[c][:].rearrange("p e t -> p (e t)"))
+            nc.vector.quantize_mx(out=x_codes[c][:].bitcast(FP8X4), scales=x_scales[c][:], in_=woven[:, chunk(c), :].rearrange("p e t -> p (e t)"))
 
         def product(sums, i, c):
             nc.tensor.matmul_mx(
@@ -134,18 +140,17 @@ def tile_picked_highway_gelu_l_kernel(tc, xT, res, w1_words, w1_scales, w2_words
             nc.tensor.matmul(sums, lhsT=source, rhs=identity[:], start=start, stop=stop, is_transpose=True)
 
         for t in range(2):
-            gather(t, woven[0][:, :, t], 0, 0, CHUNK)
-            gather(t, low_pair[:, t, :], CHUNK, CHUNK, S)
-        for c in range(1, CHUNKS):
-            place(c, 0, low_pair[:, :, chunk(c - 1)])
+            gather_direct(t)
+            gather(t, low_pair[:, t, :], DIRECT, S)
+        place("gpsimd", 384, 640, 0, low_pair[:, :, : 640 - DIRECT])
+        place("vector", 640, S, 0, low_pair[:, :, 640 - DIRECT :])
         for t in range(2, PACK):
-            gather(t, woven[0][:, :, t], 0, 0, CHUNK)
-            for c in (1, 3, 2):
-                gather(t, high_pair[c][:, t - 2, :], c * CHUNK, c * CHUNK, (c + 1) * CHUNK)
-        nc.scalar.copy(woven[3][:, :, 2:4], high_pair[3][:].rearrange("p t e -> p e t"))
+            gather_direct(t)
+            for pair, (first, end, engine) in zip(high_pair, PARTS):
+                gather(t, pair[:, t - 2, :], first, end)
+        for pair, (first, end, engine) in zip(high_pair, PARTS):
+            place(engine, first, end, 1, pair[:])
         for c in range(CHUNKS):
-            if 0 < c < 3:
-                place(c, 1, high_pair[c][:])
             quantise(c)
             product(layer_sums, 0, c)
             product(gate_sums, 1, c)

@@ -22,8 +22,8 @@ PACK = 4
 LIST_ROWS = 16
 CHUNK = 256
 CHUNKS = S // CHUNK
-DIRECT = 384
-PARTS = ((384, 512, "gpsimd"), (512, 640, "gpsimd"), (768, 1024, "scalar"), (640, 768, "vector"))
+DIRECT = 512
+PARTS = ((512, 640, "gpsimd"), (640, 768, "gpsimd"), (768, 1024, "scalar"))
 TURNED_BLOCKS = 3
 
 
@@ -76,7 +76,9 @@ def tile_picked_highway_gelu_l_kernel(tc, xT, res, w1_words, w1_scales, w2_words
             return slice(c * CHUNK, (c + 1) * CHUNK)
 
         def gather_direct(t):
-            nc.vector.tensor_copy(woven[:, :DIRECT, t], rows[t][:].indirect(entries(0, DIRECT)))
+            for first in range(0, DIRECT, CHUNK if t == PACK - 1 else DIRECT):
+                end = first + (CHUNK if t == PACK - 1 else DIRECT)
+                nc.vector.tensor_copy(woven[:, first:end, t], rows[t][:].indirect(entries(first, end)))
 
         def gather(t, plane, first, end):
             nc.scalar.activation(plane, rows[t][:].indirect(entries(first, end)), ACT.Copy)
@@ -142,8 +144,8 @@ def tile_picked_highway_gelu_l_kernel(tc, xT, res, w1_words, w1_scales, w2_words
         for t in range(2):
             gather_direct(t)
             gather(t, low_pair[:, t, :], DIRECT, S)
-        place("gpsimd", 384, 640, 0, low_pair[:, :, : 640 - DIRECT])
-        place("vector", 640, S, 0, low_pair[:, :, 640 - DIRECT :])
+        place("gpsimd", DIRECT, 768, 0, low_pair[:, :, : 768 - DIRECT])
+        place("vector", 768, S, 0, low_pair[:, :, 768 - DIRECT :])
         for t in range(2, PACK):
             gather_direct(t)
             for pair, (first, end, engine) in zip(high_pair, PARTS):

@@ -96,15 +96,17 @@ def tile_picked_highway_gelu_l_kernel(tc, xT, res, w1_words, w1_scales, w2_words
         x_scales = [keep.tile([P, CHUNK], U8, name="x_scales%d" % c, align_bytes=64) for c in range(CHUNKS)]
         layer_sums = [psum.tile([P, CHUNK], F32, name="layer_sums%d" % c, tag="layer%d" % c) for c in range(CHUNKS)]
         gate_sums = [psum.tile([P, CHUNK], F32, name="gate_sums%d" % c, tag="gate%d" % c) for c in range(CHUNKS)]
-        gate_tanh = keep.tile([P, S], F32, name="gate_tanh")
         layer = keep.tile([P, S], F32, name="layer")
         diff = keep.tile([P, S], F32, name="diff")
         gated = keep.tile([P, S], F32, name="gated")
+        early_tanh = keep.tile([P, (CHUNKS - 1) * CHUNK], F32, name="early_tanh")
         turned = keep.tile([P, TURNED_BLOCKS * P], F32, name="turned")
         result = keep.tile([P, S], F32, name="result")
 
         def block(b):
             return slice(b * P, (b + 1) * P)
+
+        gate_tanh = [early_tanh[:, chunk(c)] for c in range(CHUNKS - 1)] + [gated[:, chunk(0)]]
 
         def quantise(c):
             nc.vector.quantize_mx(out=x_codes[c][:].bitcast(FP8X4), scales=x_scales[c][:], in_=woven[:, chunk(c), :].rearrange("p e t -> p (e t)"))
@@ -124,7 +126,7 @@ def tile_picked_highway_gelu_l_kernel(tc, xT, res, w1_words, w1_scales, w2_words
             nc.scalar.activation(layer[:, chunk(c)], layer_sums[c][:], ACT.Gelu_apprx_tanh, bias=zero_bias[:] if c == 0 else 0.0)
 
         def tanh(c):
-            nc.scalar.activation(gate_tanh[:, chunk(c)], gate_sums[c][:], ACT.Tanh, scale=-0.5)
+            nc.scalar.activation(gate_tanh[c], gate_sums[c][:], ACT.Tanh, scale=-0.5)
 
         def subtract(c):
             cols = chunk(c)
@@ -132,7 +134,7 @@ def tile_picked_highway_gelu_l_kernel(tc, xT, res, w1_words, w1_scales, w2_words
 
         def gate(c):
             cols = chunk(c)
-            nc.vector.scalar_tensor_tensor(gated[:, cols], gate_tanh[:, cols], 1.0, diff[:, cols], ALU.add, ALU.mult)
+            nc.vector.scalar_tensor_tensor(gated[:, cols], gate_tanh[c], 1.0, diff[:, cols], ALU.add, ALU.mult)
 
         def finish(cols):
             nc.vector.scalar_tensor_tensor(result[:, cols], gated[:, cols], 0.5, layer[:, cols], ALU.mult, ALU.add)
@@ -156,10 +158,8 @@ def tile_picked_highway_gelu_l_kernel(tc, xT, res, w1_words, w1_scales, w2_words
             quantise(c)
             product(layer_sums, 0, c)
             product(gate_sums, 1, c)
-        for pair in ((0, 1), (2, 3)):
-            for step in (gelu, tanh):
-                for c in pair:
-                    step(c)
+        for step, c in ((gelu, 0), (gelu, 1), (tanh, 0), (tanh, 1), (gelu, 2), (gelu, 3), (tanh, 2)):
+            step(c)
 
         turned_sums = [psum.tile([P, P], F32, name="turned_sums%d" % b, tag="layer%d" % b) for b in range(TURNED_BLOCKS)]
         for b in range(TURNED_BLOCKS):
@@ -171,6 +171,7 @@ def tile_picked_highway_gelu_l_kernel(tc, xT, res, w1_words, w1_scales, w2_words
         for b in range(TURNED_BLOCKS):
             turn(turned_sums[b][:], gated[:, block(b)], False, True)
             nc.scalar.activation(turned[:, block(b)], turned_sums[b][:], ACT.Copy, scale=0.5)
+        tanh(3)
         for c in range(2):
             first, end = c * CHUNK, min((c + 1) * CHUNK, TURNED_BLOCKS * P)
             result_sums = psum.tile([P, end - first], F32, name="result_sums%d" % c, tag="gate%d" % c)

@@ -23,7 +23,7 @@ LIST_ROWS = 16
 CHUNK = 256
 CHUNKS = S // CHUNK
 DIRECT = 512
-PARTS = ((512, 640, "gpsimd"), (640, 768, "gpsimd"), (768, 1024, "scalar"))
+PARTS = ((512, 576, "gpsimd"), (576, 768, "gpsimd"), (768, 1024, "scalar"))
 TURNED_BLOCKS = 3
 
 

@@ -23,7 +23,7 @@ LIST_ROWS = 16
 CHUNK = 256
 CHUNKS = S // CHUNK
 DIRECT = 512
-PARTS = ((512, 576, "gpsimd"), (576, 768, "gpsimd"), (768, 1024, "scalar"))
+PARTS = ((512, 576, "gpsimd"), (576, 704, "gpsimd"), (704, 768, "scalar"), (768, 1024, "scalar"))
 TURNED_BLOCKS = 3
 
 

from contextlib import ExitStack

import concourse.mybir as mybir
from concourse.masks import make_identity

K, T, S, N = 512, 2048, 1024, 128
FLOPS = 2 * 2 * K * S * N

F32 = mybir.dt.float32
BF16 = mybir.dt.bfloat16
I32 = mybir.dt.int32
U32 = mybir.dt.uint32
U16 = mybir.dt.uint16
U8 = mybir.dt.uint8
FP8X4 = mybir.dt.float8_e4m3fn_x4
FP4X4 = mybir.dt.float4_e2m1fn_x4
ACT = mybir.ActivationFunctionType
ALU = mybir.AluOpType

P = 128
PACK = 4
LIST_ROWS = 16
CHUNK = 256
CHUNKS = S // CHUNK
DIRECT = 512
PARTS = ((512, 576, "gpsimd"), (576, 704, "gpsimd"), (704, 768, "scalar"), (768, 1024, "scalar"))
TURNED_BLOCKS = 3


def tile_picked_highway_gelu_l_kernel(tc, xT, res, w1_words, w1_scales, w2_words, w2_scales, offs, out):
    nc = tc.nc
    x_rows = xT.rearrange("(p t) c -> p t c", t=PACK)

    with ExitStack() as ctx:
        keep = ctx.enter_context(tc.tile_pool(name="keep", bufs=1))
        psum = ctx.enter_context(tc.psum_pool(name="psum", bufs=1))

        offsets = keep.tile([P, S // LIST_ROWS], U16, name="offsets")
        res_sb = keep.tile([P, T], F32, name="res_sb")
        w_words = [keep.tile([P, 2 * N], U8, name="w_words%d" % i, align_bytes=64) for i in range(2)]
        w_scales = [keep.tile([P, N], U8, name="w_scales%d" % i, align_bytes=64) for i in range(2)]
        rows = [keep.tile([P, T], F32, name="row%d" % t) for t in range(PACK)]
        low_pair = keep.tile([P, 2, S - DIRECT], BF16, name="low_pair")
        high_pair = [keep.tile([P, 2, end - first], BF16, name="high_pair%d" % first) for first, end, engine in PARTS]
        woven = keep.tile([P, S, PACK], BF16, name="woven", align_bytes=64)
        zero = keep.tile([P, 1], F32, name="zero")
        zero_bias = keep.tile([P, 1], F32, name="zero_bias")
        identity = keep.tile([P, P], F32, name="identity")

        nc.vector.memset(zero[:], 0.0)
        nc.scalar.activation(zero_bias[:], zero[:], ACT.Gelu_apprx_tanh)

        def load_scales(queue, i, dram):
            for q in range(4):
                queue.dma_start(
                    out=w_scales[i][32 * q : 32 * q + 4, :].bitcast(I32),
                    in_=dram[0][4 * q : 4 * q + 4, :].bitcast(I32),
                )

        for t in range(PACK):
            nc.sync.dma_start(out=rows[t][:], in_=x_rows[:, t, :])
            if t == 0:
                nc.sync.dma_start(offsets[:], offs)
                load_scales(nc.sync, 0, w1_scales)
            if t == 2:
                load_scales(nc.sync, 1, w2_scales)
        for tile, dram in zip(w_words, (w1_words, w2_words)):
            nc.sync.dma_start(out=tile[:].bitcast(I32), in_=dram[0].bitcast(I32))
        nc.sync.dma_start(out=res_sb[:], in_=res)
        make_identity(nc, identity[:])

        def entries(first, end):
            return offsets[:, first // LIST_ROWS : end // LIST_ROWS]

        def chunk(c):
            return slice(c * CHUNK, (c + 1) * CHUNK)

        def gather_direct(t):
            for first in range(0, DIRECT, CHUNK if t == PACK - 1 else DIRECT):
                end = first + (CHUNK if t == PACK - 1 else DIRECT)
                nc.vector.tensor_copy(woven[:, first:end, t], rows[t][:].indirect(entries(first, end)))

        def gather(t, plane, first, end):
            nc.scalar.activation(plane, rows[t][:].indirect(entries(first, end)), ACT.Copy)

        def place(engine, first, end, half, pair):
            target, source = woven[:, first:end, 2 * half : 2 * half + 2], pair.rearrange("p t e -> p e t")
            if engine == "gpsimd":
                nc.gpsimd.tensor_scalar(target, source, 1.0, 0.0, ALU.mult, ALU.add)
            elif engine == "scalar":
                nc.scalar.copy(target, source)
            else:
                nc.vector.tensor_copy(target, source)

        x_codes = [keep.tile([P, CHUNK], U32, name="x_codes%d" % c, align_bytes=64) for c in range(CHUNKS)]
        x_scales = [keep.tile([P, CHUNK], U8, name="x_scales%d" % c, align_bytes=64) for c in range(CHUNKS)]
        layer_sums = [psum.tile([P, CHUNK], F32, name="layer_sums%d" % c, tag="layer%d" % c) for c in range(CHUNKS)]
        gate_sums = [psum.tile([P, CHUNK], F32, name="gate_sums%d" % c, tag="gate%d" % c) for c in range(CHUNKS)]
        layer = keep.tile([P, S], F32, name="layer")
        diff = keep.tile([P, S], F32, name="diff")
        gated = keep.tile([P, S], F32, name="gated")
        early_tanh = keep.tile([P, (CHUNKS - 1) * CHUNK], F32, name="early_tanh")
        turned = keep.tile([P, TURNED_BLOCKS * P], F32, name="turned")
        result = keep.tile([P, S], F32, name="result")

        def block(b):
            return slice(b * P, (b + 1) * P)

        gate_tanh = [early_tanh[:, chunk(c)] for c in range(CHUNKS - 1)] + [gated[:, chunk(0)]]

        def quantise(c):
            nc.vector.quantize_mx(out=x_codes[c][:].bitcast(FP8X4), scales=x_scales[c][:], in_=woven[:, chunk(c), :].rearrange("p e t -> p (e t)"))

        def product(sums, i, c):
            nc.tensor.matmul_mx(
                out=sums[c][:],
                lhsT=w_words[i][:].bitcast(FP4X4),
                lhsT_scale=w_scales[i][:],
                rhs=x_codes[c][:].bitcast(FP8X4),
                rhs_scale=x_scales[c][:],
                start=True,
                stop=True,
            )

        def gelu(c):
            nc.scalar.activation(layer[:, chunk(c)], layer_sums[c][:], ACT.Gelu_apprx_tanh, bias=zero_bias[:] if c == 0 else 0.0)

        def tanh(c):
            nc.scalar.activation(gate_tanh[c], gate_sums[c][:], ACT.Tanh, scale=-0.5)

        def subtract(c):
            cols = chunk(c)
            nc.vector.tensor_tensor(diff[:, cols], res_sb[:].indirect(entries(cols.start, cols.stop)), layer[:, cols], ALU.subtract)

        def gate(c):
            cols = chunk(c)
            nc.vector.scalar_tensor_tensor(gated[:, cols], gate_tanh[c], 1.0, diff[:, cols], ALU.add, ALU.mult)

        def finish(cols):
            nc.vector.scalar_tensor_tensor(result[:, cols], gated[:, cols], 0.5, layer[:, cols], ALU.mult, ALU.add)
            nc.sync.dma_start(out=out[:, cols], in_=result[:, cols])

        def turn(sums, source, start, stop):
            nc.tensor.matmul(sums, lhsT=source, rhs=identity[:], start=start, stop=stop, is_transpose=True)

        for t in range(2):
            gather_direct(t)
            gather(t, low_pair[:, t, :], DIRECT, S)
        place("gpsimd", DIRECT, 768, 0, low_pair[:, :, : 768 - DIRECT])
        place("vector", 768, S, 0, low_pair[:, :, 768 - DIRECT :])
        for t in range(2, PACK):
            gather_direct(t)
            for pair, (first, end, engine) in zip(high_pair, PARTS):
                gather(t, pair[:, t - 2, :], first, end)
        for pair, (first, end, engine) in zip(high_pair, PARTS):
            place(engine, first, end, 1, pair[:])
        for c in range(CHUNKS):
            quantise(c)
            product(layer_sums, 0, c)
            product(gate_sums, 1, c)
        for step, c in ((gelu, 0), (gelu, 1), (tanh, 0), (tanh, 1), (gelu, 2), (gelu, 3), (tanh, 2)):
            step(c)

        turned_sums = [psum.tile([P, P], F32, name="turned_sums%d" % b, tag="layer%d" % b) for b in range(TURNED_BLOCKS)]
        for b in range(TURNED_BLOCKS):
            turn(turned_sums[b][:], layer[:, block(b)], True, False)
            turn(turned_sums[b][:], layer[:, block(b)], False, False)
        for step in (subtract, gate):
            step(0)
            step(1)
        for b in range(TURNED_BLOCKS):
            turn(turned_sums[b][:], gated[:, block(b)], False, True)
            nc.scalar.activation(turned[:, block(b)], turned_sums[b][:], ACT.Copy, scale=0.5)
        tanh(3)
        for c in range(2):
            first, end = c * CHUNK, min((c + 1) * CHUNK, TURNED_BLOCKS * P)
            result_sums = psum.tile([P, end - first], F32, name="result_sums%d" % c, tag="gate%d" % c)
            for b in range(first // P, end // P):
                turn(result_sums[:, b * P - first : (b + 1) * P - first], turned[:, block(b)], True, True)
            nc.scalar.copy(result[:, first:end], result_sums[:])
            nc.scalar.dma_start(out=out[:, first:end], in_=result[:, first:end])
        subtract(2)
        finish(slice(TURNED_BLOCKS * P, 2 * CHUNK))
        subtract(3)
        gate(2)
        gate(3)
        finish(chunk(2))
        finish(chunk(3))
